import numpy as np
import ml_dtypes


def mxq(x, axis, fmt="e4m3"):
    dtype, down = {"e4m3": (ml_dtypes.float8_e4m3fn, 7), "e5m2": (ml_dtypes.float8_e5m2, 14)}[fmt]
    v = np.moveaxis(np.asarray(x, np.float32).astype(ml_dtypes.bfloat16).astype(np.float64), axis, -1)
    blocks = v.reshape(v.shape[:-1] + (-1, 32))
    amax = np.abs(blocks).max(-1, keepdims=True)
    byte = np.maximum(np.where(amax > 0, np.frexp(amax)[1] - 1 + 127, 0) - down, 1)
    scale = np.exp2(byte - 127.0)
    codes = (blocks / scale).astype(np.float32).astype(dtype).astype(np.float64)
    return np.moveaxis((codes * scale).reshape(v.shape), -1, axis)


WIDE = False


def mx_kscale(k):
    if not WIDE:
        return np.ones(k)
    levels = np.array([10, -10, 5, -5, 0])
    if k % 512:
        return np.exp2(np.random.permutation(np.resize(levels, k // 32))).repeat(32)
    a = np.empty((k // 512, 16))
    for p in range(k // 512):
        a[p, :8] = np.random.permutation(np.resize(levels, 8))
        for g in range(8):
            far = levels[np.abs(levels - a[p, g]) >= 10]
            a[p, g + 8] = far[np.random.randint(len(far))]
    return np.exp2(a.ravel()).repeat(32)


def f64(x):
    return np.asarray(x).astype(np.float64)


def striped(idx):
    return np.tile(idx.reshape(-1, 16).T, (8, 1)).astype(np.uint16)


def unstriped(offs):
    return offs[:16].T.reshape(-1).astype(np.int64)


E2M1 = np.array([0.0, 0.5, 1.0, 1.5, 2.0, 3.0, 4.0, 6.0, -0.0, -0.5, -1.0, -1.5, -2.0, -3.0, -4.0, -6.0])


def pack_weight(w, fmt):
    k, n = w.shape
    w = f64(np.asarray(w, np.float32).astype(ml_dtypes.bfloat16)).reshape(k // 32, 32, n)
    amax = np.abs(w).max(1)
    if fmt == "e4m3":
        byte = np.frexp(amax)[1] - 1 + 127 - 7
    else:
        mant, ex = np.frexp(amax / 6.0)
        byte = np.where(mant > 0.5, ex, ex - 1) + 127
    byte = np.clip(np.where(amax > 0, byte, 1), 1, 254)
    scaled = (w * np.exp2(127.0 - byte)[:, None, :]).reshape(k, n).astype(np.float32)
    by_word = np.ascontiguousarray(scaled.reshape(k // 512, 128, 4, n).transpose(0, 1, 3, 2))
    if fmt == "e4m3":
        words = by_word.astype(ml_dtypes.float8_e4m3fn).view(np.uint8)
    else:
        c = by_word.astype(ml_dtypes.float4_e2m1fn).view(np.uint8) & 0xF
        words = (c[..., 0::2] | (c[..., 1::2] << 4)).reshape(k // 512, 128, 2 * n)
    return np.ascontiguousarray(words), np.ascontiguousarray(byte.astype(np.uint8).reshape(k // 512, 16, n))


def unpack_weight(words, scales, fmt):
    g, _, n = scales.shape
    words = np.ascontiguousarray(words).reshape(g, 128, n, -1)
    if fmt == "e4m3":
        vals = words.view(ml_dtypes.float8_e4m3fn).astype(np.float64)
    else:
        nib = np.empty((g, 128, n, 4), np.uint8)
        nib[..., 0::2] = words & 0xF
        nib[..., 1::2] = words >> 4
        vals = E2M1[nib]
    vals = vals * np.repeat(np.exp2(scales.astype(np.float64) - 127.0), 8, axis=1)[..., None]
    return vals.transpose(0, 1, 3, 2).reshape(g * 512, n)


def gelu(v):
    return 0.5 * v * (1.0 + np.tanh(np.sqrt(2.0 / np.pi) * (v + 0.044715 * v**3)))


K, T, S, H, N = 1024, 2048, 1024, 512, 256

def setup_inputs():
    n = np.random.standard_normal
    s = mx_kscale(K)[:, None]
    u = mx_kscale(H)[:, None]
    tab_words, tab_scales = pack_weight(n((K, T)) * s, "e4m3")
    w1 = (n((K, H)) / np.sqrt(K) / s * u.T).astype(np.float32)
    w2_words, w2_scales = pack_weight(n((K, H)) / np.sqrt(K) / s * u.T, "e4m3")
    w3_words, w3_scales = pack_weight(n((K, H)) / np.sqrt(K) / s * u.T, "e2m1")
    bh = (0.5 * n(H) * u[:, 0]).astype(np.float32)
    wo = (n((H, N)) / np.sqrt(H) / u).astype(np.float32)
    bo = (0.5 * n(N)).astype(np.float32)
    offs = striped(np.random.permutation(T)[:S])
    return {"tab_words": tab_words, "tab_scales": tab_scales, "offs": offs, "w1": w1,
            "w2_words": w2_words, "w2_scales": w2_scales, "w3_words": w3_words,
            "w3_scales": w3_scales, "bh": bh, "wo": wo, "bo": bo}

def reference(tab_words, tab_scales, offs, w1, w2_words, w2_scales, w3_words, w3_scales, bh, wo, bo):
    v = unpack_weight(tab_words, tab_scales, "e4m3")[:, unstriped(offs)]
    a = mxq(f64(w1), 0, "e4m3").T @ v
    b = unpack_weight(w2_words, w2_scales, "e4m3").T @ v
    c = unpack_weight(w3_words, w3_scales, "e2m1").T @ v
    h = np.maximum(np.maximum(a, b), c) + f64(bh)[:, None]
    y = mxq(f64(wo), 0, "e4m3").T @ mxq(h, 0, "e4m3")
    return y + f64(bo)[:, None]

@@ -1,0 +1,265 @@
+from contextlib import ExitStack
+
+import concourse.mybir as mybir
+
+K, T, S, H, N = 1024, 2048, 1024, 512, 256
+FLOPS = 2 * 3 * K * H * S + 2 * H * N * S
+
+F32 = mybir.dt.float32
+BF16 = mybir.dt.bfloat16
+I32 = mybir.dt.int32
+U32 = mybir.dt.uint32
+U16 = mybir.dt.uint16
+U8 = mybir.dt.uint8
+FP8X4 = mybir.dt.float8_e4m3fn_x4
+FP4X4 = mybir.dt.float4_e2m1fn_x4
+ADD = mybir.AluOpType.add
+MAX = mybir.AluOpType.max
+MULT = mybir.AluOpType.mult
+IDENT = mybir.ActivationFunctionType.Identity
+
+P = 128
+PACK = 4
+PASSES = K // (P * PACK)
+RUN = 8
+HALF = 512
+HALVES = S // HALF
+PIECE = 256
+LAG = 2
+
+
+def tile_list_pocket_max_affinity_kernel(
+    tc, tab_words, tab_scales, offs, w1, w2_words, w2_scales, w3_words, w3_scales, bh, wo, bo, out
+):
+    nc = tc.nc
+    with ExitStack() as ctx:
+        keep = ctx.enter_context(tc.tile_pool(name="keep", bufs=1))
+        stage = ctx.enter_context(tc.tile_pool(name="stage", bufs=1))
+        psum = ctx.enter_context(tc.psum_pool(name="psum", bufs=8))
+
+        def sb(shape, dtype, name):
+            return keep.tile(shape, dtype, name=name, align_bytes=64)
+
+        def load_scales(queue, plane, scales):
+            rows = scales.bitcast(I32).rearrange("a (g r) w -> r g a w", r=4)
+            for r in range(4):
+                queue.dma_start(out=plane[r:P:32, :, :].bitcast(I32), in_=rows[r])
+
+        def regroup(dst, src):
+            for a in range(PASSES):
+                nc.vector.tensor_copy(
+                    out=dst[:, a, :].bitcast(I32).rearrange("p (t q w) -> p t q w", t=PACK, q=16),
+                    in_=src[:, a, :].bitcast(I32).rearrange("p (q t w) -> p t q w", t=PACK, q=16),
+                )
+
+        offsets = keep.tile([P, S // 16], U16, name="offsets")
+        nc.sync.dma_start(offsets[:], offs)
+
+        tab_plane = stage.tile([P, T], U8, name="tab_plane", offset=24576 + 1024)
+        nc.vector.memset(tab_plane[:].bitcast(I32), 0)
+        for g in range(4):
+            nc.scalar.dma_start(
+                out=tab_plane[32 * g : 32 * g + 8, :].bitcast(I32),
+                in_=tab_scales.bitcast(I32)[:, 4 * g : 4 * g + 4, :],
+            )
+        w2_plane_raw = stage.tile([P, PASSES, H], U8, name="w2_plane_raw", offset=16384)
+        w3_plane_raw = sb([P, PASSES, H], U8, "w3_plane_raw")
+        nc.gpsimd.memset(w2_plane_raw[:].bitcast(I32), 0)
+        load_scales(nc.gpsimd, w2_plane_raw, w2_scales)
+        nc.vector.memset(w3_plane_raw[:].bitcast(I32), 0)
+        load_scales(nc.scalar, w3_plane_raw, w3_scales)
+        v_plane_low = sb([P, S], U8, "v_plane_low")
+        nc.vector.memset(v_plane_low[:].bitcast(I32), 0)
+
+        w2_raw = stage.tile([P, PASSES, 4 * H], U8, name="w2_raw", offset=8192 - 64)
+        nc.sync.dma_start(
+            out=w2_raw[:].bitcast(I32), in_=w2_words.rearrange("a p e i -> p a (e i)").bitcast(I32)
+        )
+        tab = [sb([P, T], I32, f"tab{a}") for a in range(PASSES)]
+        for a in range(PASSES):
+            nc.sync.dma_start(out=tab[a][:], in_=tab_words[a].rearrange("p t i -> p (t i)").bitcast(I32))
+
+        bh_cols = [sb([P, 1], F32, f"bh_col{t}") for t in range(PACK)]
+        bo_col = sb([P, N // P], F32, "bo_col")
+        with nc.allow_non_contiguous_dma(reason="one bias value a partition"):
+            bh_rows = bh.rearrange("(q t i o) -> t q i o", t=PACK, i=RUN, o=1)
+            for t in range(PACK):
+                nc.gpsimd.dma_start(out=bh_cols[t][:], in_=bh_rows[t])
+            nc.gpsimd.dma_start(out=bo_col[:], in_=bo.rearrange("(u p) -> p u", p=P))
+
+        w2_codes = sb([P, PASSES, 4 * H], U8, "w2_codes")
+        w2_plane = sb([P, PASSES, H], U8, "w2_plane")
+        regroup(w2_codes, w2_raw)
+        regroup(w2_plane, w2_plane_raw)
+
+        w3_raw = stage.tile([P, PASSES, 2 * H], U8, name="w3_raw", offset=12288 - 128)
+        nc.sync.dma_start(out=w3_raw[:].bitcast(I32), in_=w3_words.rearrange("a p b -> p a b").bitcast(I32))
+        w1_raw = [
+            stage.tile([P, PACK, H], F32, name=f"w1_raw{a}", offset=(0, 16384)[a]) for a in range(PASSES)
+        ]
+        for a in range(PASSES):
+            nc.sync.dma_start(
+                out=w1_raw[a][:], in_=w1[a * 512 : (a + 1) * 512, :].rearrange("(p j) c -> p j c", j=PACK)
+            )
+
+        v_plane = sb([P, S], U8, "v_plane")
+        picks = [offsets[:, s * HALF // 16 : (s + 1) * HALF // 16] for s in range(HALVES)]
+        for s in range(HALVES):
+            nc.vector.tensor_copy(v_plane[:, s * HALF : (s + 1) * HALF], tab_plane[:].indirect(picks[s]))
+        for r in range(4):
+            nc.scalar.dma_start(out=v_plane_low[r:P:32, :].bitcast(I32), in_=v_plane[4 + r : P : 32, :].bitcast(I32))
+        v_codes = [
+            [
+                stage.tile([P, HALF], U32, name=f"v_codes{a}_{s}", offset=24576 + 2048 * (2 * a + s), align_bytes=64)
+                for s in range(HALVES)
+            ]
+            for a in range(PASSES)
+        ]
+        for a in range(PASSES):
+            for s in range(HALVES):
+                nc.vector.tensor_copy(v_codes[a][s][:], tab[a][:].bitcast(U32).indirect(picks[s]))
+
+        w3_codes = sb([P, PASSES, 2 * H], U8, "w3_codes")
+        w3_plane = sb([P, PASSES, H], U8, "w3_plane")
+        regroup(w3_codes, w3_raw)
+        regroup(w3_plane, w3_plane_raw)
+
+        wo_raw = stage.tile([P, PACK, N], F32, name="wo_raw", offset=12288 - 64)
+        wo_rows = wo.rearrange("(q t i) n -> t q i n", t=PACK, i=RUN)
+        for t in range(PACK):
+            nc.sync.dma_start(out=wo_raw[:, t, :], in_=wo_rows[t])
+
+        def product(acc, codes, plane, a, j0, width, low=False):
+            s, c0 = divmod(j0, HALF)
+            cols = slice(j0, j0 + width)
+            scale = v_plane_low[:, cols] if low and a == 1 else v_plane[4 * a : P, cols]
+            nc.tensor.matmul_mx(
+                out=acc[:, :width],
+                lhsT=codes,
+                lhsT_scale=plane,
+                rhs=v_codes[a][s][:, c0 : c0 + width].bitcast(FP8X4),
+                rhs_scale=scale,
+                start=(a == 0),
+                stop=(a == PASSES - 1),
+            )
+
+        units = [(s, t) for s in range(HALVES) for t in range(PACK)]
+        acc_b = {u: psum.tile([P, HALF], F32, name="acc") for u in units}
+        for a in range(PASSES):
+            for s, t in units:
+                product(
+                    acc_b[s, t],
+                    w2_codes[:, a, t * 512 : (t + 1) * 512].bitcast(FP8X4),
+                    w2_plane[:, a, t * P : (t + 1) * P],
+                    a, s * HALF, HALF,
+                )
+        b_sb = {(s, t): sb([P, HALF], F32, f"b_sb{s}_{t}") for s, t in units}
+        for s, t in units:
+            nc.scalar.activation(b_sb[s, t][:], acc_b[s, t][:], IDENT, bias=bh_cols[t][:])
+
+        w1_bf = [sb([P, PACK, 16, RUN, PACK], BF16, f"w1_bf{a}") for a in range(PASSES)]
+        w1_codes = [sb([P, H], U32, f"w1_codes{a}") for a in range(PASSES)]
+        w1_plane = [sb([P, H], U8, f"w1_plane{a}") for a in range(PASSES)]
+
+        def cast_w1(a, t):
+            src = w1_raw[a][:].rearrange("p j (q t i) -> p t q i j", t=PACK, i=RUN)[:, t]
+            dst = w1_bf[a][:, t]
+            if a == 1 and t % 2 == 1:
+                nc.scalar.copy(out=dst.rearrange("p q i j -> p q j i"), in_=src.rearrange("p q i j -> p q j i"))
+            else:
+                nc.gpsimd.tensor_scalar(dst, src, 1.0, 0.0, MULT, ADD)
+
+        def quantize_w1(a):
+            nc.vector.quantize_mx(
+                out=w1_codes[a][:].bitcast(FP8X4),
+                scales=w1_plane[a][:],
+                in_=w1_bf[a][:].rearrange("p t q i j -> p (t q i j)"),
+            )
+
+        for a in range(PASSES):
+            for t in range(PACK):
+                cast_w1(a, t)
+
+        bc_sb = {(s, t): sb([P, HALF], F32, f"bc_sb{s}_{t}") for s, t in units}
+        for s, t in units:
+            acc = psum.tile([P, HALF], F32, name="acc")
+            for a in range(PASSES):
+                product(
+                    acc,
+                    w3_codes[:, a, t * 256 : (t + 1) * 256].bitcast(FP4X4),
+                    w3_plane[:, a, t * P : (t + 1) * P],
+                    a, s * HALF, HALF, low=True,
+                )
+            nc.vector.scalar_tensor_tensor(
+                bc_sb[s, t][:], acc[:], bh_cols[t][:], b_sb[s, t][:], ADD, MAX
+            )
+            if t == PACK - 1:
+                quantize_w1(s)
+
+        wo_bf = sb([P, N, PACK], BF16, "wo_bf")
+        wo_codes = sb([P, N], U32, "wo_codes")
+        wo_plane = sb([P, N], U8, "wo_plane")
+        for u in range(N // P):
+            cols = slice(u * P, (u + 1) * P)
+            nc.gpsimd.tensor_scalar(
+                wo_bf[:, cols, :], wo_raw[:, :, cols].rearrange("p t n -> p n t"), 1.0, 0.0, MULT, ADD
+            )
+        nc.vector.quantize_mx(
+            out=wo_codes[:].bitcast(FP8X4), scales=wo_plane[:], in_=wo_bf[:].rearrange("p n t -> p (n t)")
+        )
+
+        out_rows = out.rearrange("(u p) s -> p u s", p=P)
+
+        def second_product(h_rows, c0, j0):
+            h_bf = sb([P, PIECE, PACK], BF16, f"h_bf{j0}")
+            nc.scalar.copy(
+                out=h_bf[:].rearrange("p (c i) t -> p c t i", i=4),
+                in_=h_rows[:, :, c0 : c0 + PIECE].rearrange("p t (c i) -> p c t i", i=4),
+            )
+            h_codes = sb([P, PIECE], U32, f"h_codes{j0}")
+            h_plane = sb([P, PIECE], U8, f"h_plane{j0}")
+            nc.vector.quantize_mx(
+                out=h_codes[:].bitcast(FP8X4), scales=h_plane[:], in_=h_bf[:].rearrange("p n t -> p (n t)")
+            )
+            acc = psum.tile([P, HALF], F32, name="acc")
+            y = sb([P, N // P, PIECE], F32, f"y{j0}")
+            for u in range(N // P):
+                nc.tensor.matmul_mx(
+                    out=acc[:, u * PIECE : (u + 1) * PIECE],
+                    lhsT=wo_codes[:, u * P : (u + 1) * P].bitcast(FP8X4),
+                    lhsT_scale=wo_plane[:, u * P : (u + 1) * P],
+                    rhs=h_codes[:].bitcast(FP8X4),
+                    rhs_scale=h_plane[:],
+                    start=True,
+                    stop=True,
+                )
+            for u in range(N // P):
+                nc.scalar.activation(
+                    y[:, u, :], acc[:, u * PIECE : (u + 1) * PIECE], IDENT, bias=bo_col[:, u : u + 1]
+                )
+            nc.sync.dma_start(out=out_rows[:, :, j0 : j0 + PIECE], in_=y[:])
+
+        def third_pocket(j0):
+            s, c0 = divmod(j0, HALF)
+            h_rows = sb([P, PACK, PIECE], BF16, f"h_rows{j0}")
+            for t in range(PACK):
+                acc = psum.tile([P, HALF], F32, name="acc")
+                for a in range(PASSES):
+                    product(
+                        acc,
+                        w1_codes[a][:, t * P : (t + 1) * P].bitcast(FP8X4),
+                        w1_plane[a][:, t * P : (t + 1) * P],
+                        a, j0, PIECE,
+                    )
+                nc.vector.scalar_tensor_tensor(
+                    h_rows[:, t, :], acc[:, :PIECE], bh_cols[t][:], bc_sb[s, t][:, c0 : c0 + PIECE], ADD, MAX
+                )
+            return h_rows
+
+        starts = list(range(0, S, PIECE))
+        rows = {}
+        for n in range(len(starts) + LAG):
+            if n < len(starts):
+                rows[n] = third_pocket(starts[n])
+            if n >= LAG:
+                second_product(rows[n - LAG], 0, starts[n - LAG])

@@ -24,8 +24,9 @@ PASSES = K // (P * PACK)
 RUN = 8
 HALF = 512
 HALVES = S // HALF
-PIECE = 256
-LAG = 2
+LAG = 1
+PIECES = [(0, 256), (256, 256), (512, 256), (768, 128), (896, 128)]
+KIB = 1024
 
 
 def tile_list_pocket_max_affinity_kernel(
@@ -35,15 +36,18 @@ def tile_list_pocket_max_affinity_kernel(
     with ExitStack() as ctx:
         keep = ctx.enter_context(tc.tile_pool(name="keep", bufs=1))
         stage = ctx.enter_context(tc.tile_pool(name="stage", bufs=1))
-        psum = ctx.enter_context(tc.psum_pool(name="psum", bufs=8))
+        psum = ctx.enter_context(tc.psum_pool(name="psum", bufs=1))
 
         def sb(shape, dtype, name):
             return keep.tile(shape, dtype, name=name, align_bytes=64)
 
-        def load_scales(queue, plane, scales):
+        def bank(n, name):
+            return psum.tile([P, HALF], F32, name=name, offset=2 * KIB * n)
+
+        def load_scales(plane, scales):
             rows = scales.bitcast(I32).rearrange("a (g r) w -> r g a w", r=4)
             for r in range(4):
-                queue.dma_start(out=plane[r:P:32, :, :].bitcast(I32), in_=rows[r])
+                nc.sync.dma_start(out=plane[r:P:32, :, :].bitcast(I32), in_=rows[r])
 
         def regroup(dst, src):
             for a in range(PASSES):
@@ -55,66 +59,70 @@ def tile_list_pocket_max_affinity_kernel(
         offsets = keep.tile([P, S // 16], U16, name="offsets")
         nc.sync.dma_start(offsets[:], offs)
 
-        tab_plane = stage.tile([P, T], U8, name="tab_plane", offset=24576 + 1024)
-        nc.vector.memset(tab_plane[:].bitcast(I32), 0)
+        tab_plane = sb([P, T], U8, "tab_plane")
+        w2_plane_raw = sb([P, PASSES, H], U8, "w2_plane_raw")
+        w3_plane_raw = sb([P, PASSES, H], U8, "w3_plane_raw")
+        v_plane_low = sb([P, S], U8, "v_plane_low")
+        nc.gpsimd.memset(tab_plane[:].bitcast(I32), 0)
+        nc.gpsimd.memset(w2_plane_raw[:].bitcast(I32), 0)
+        nc.vector.memset(w3_plane_raw[:].bitcast(I32), 0)
+        nc.vector.memset(v_plane_low[:].bitcast(I32), 0)
+        warm = sb([P, 16], F32, "warm")
+        nc.vector.memset(warm[:, 0:8], 0.0)
+        nc.scalar.activation(warm[:, 8:16], warm[:, 0:8], IDENT)
+
         for g in range(4):
-            nc.scalar.dma_start(
+            nc.sync.dma_start(
                 out=tab_plane[32 * g : 32 * g + 8, :].bitcast(I32),
                 in_=tab_scales.bitcast(I32)[:, 4 * g : 4 * g + 4, :],
             )
-        w2_plane_raw = stage.tile([P, PASSES, H], U8, name="w2_plane_raw", offset=16384)
-        w3_plane_raw = sb([P, PASSES, H], U8, "w3_plane_raw")
-        nc.gpsimd.memset(w2_plane_raw[:].bitcast(I32), 0)
-        load_scales(nc.gpsimd, w2_plane_raw, w2_scales)
-        nc.vector.memset(w3_plane_raw[:].bitcast(I32), 0)
-        load_scales(nc.scalar, w3_plane_raw, w3_scales)
-        v_plane_low = sb([P, S], U8, "v_plane_low")
-        nc.vector.memset(v_plane_low[:].bitcast(I32), 0)
-
-        w2_raw = stage.tile([P, PASSES, 4 * H], U8, name="w2_raw", offset=8192 - 64)
+        w2_raw = sb([P, PASSES, 4 * H], U8, "w2_raw")
         nc.sync.dma_start(
             out=w2_raw[:].bitcast(I32), in_=w2_words.rearrange("a p e i -> p a (e i)").bitcast(I32)
         )
-        tab = [sb([P, T], I32, f"tab{a}") for a in range(PASSES)]
-        for a in range(PASSES):
-            nc.sync.dma_start(out=tab[a][:], in_=tab_words[a].rearrange("p t i -> p (t i)").bitcast(I32))
-
+        tab_rows = tab_words.rearrange("a p t i -> a p (t i)").bitcast(I32)
+        tab = [stage.tile([P, T], I32, name=f"tab{a}", offset=8 * KIB * a) for a in range(PASSES)]
+        load_scales(w2_plane_raw, w2_scales)
+        nc.sync.dma_start(out=tab[0][:], in_=tab_rows[0])
+        nc.sync.dma_start(out=tab[1][:], in_=tab_rows[1])
+        w3_raw = sb([P, PASSES, 2 * H], U8, "w3_raw")
+        nc.sync.dma_start(out=w3_raw[:].bitcast(I32), in_=w3_words.rearrange("a p b -> p a b").bitcast(I32))
         bh_cols = [sb([P, 1], F32, f"bh_col{t}") for t in range(PACK)]
-        bo_col = sb([P, N // P], F32, "bo_col")
         with nc.allow_non_contiguous_dma(reason="one bias value a partition"):
             bh_rows = bh.rearrange("(q t i o) -> t q i o", t=PACK, i=RUN, o=1)
             for t in range(PACK):
-                nc.gpsimd.dma_start(out=bh_cols[t][:], in_=bh_rows[t])
-            nc.gpsimd.dma_start(out=bo_col[:], in_=bo.rearrange("(u p) -> p u", p=P))
+                nc.sync.dma_start(out=bh_cols[t][:], in_=bh_rows[t])
+
+        w1_rows = w1.rearrange("(a p j) c -> a p j c", p=P, j=PACK)
+        w1_raw = [sb([P, PACK, H], F32, f"w1_raw{a}") for a in range(PASSES)]
+        nc.sync.dma_start(out=w1_raw[0][:], in_=w1_rows[0])
+
+        picks = [offsets[:, s * HALF // 16 : (s + 1) * HALF // 16] for s in range(HALVES)]
+        v_plane = sb([P, S], U8, "v_plane")
+        for s in range(HALVES):
+            nc.vector.tensor_copy(v_plane[:, s * HALF : (s + 1) * HALF], tab_plane[:].indirect(picks[s]))
+        nc.scalar.dma_start(out=v_plane_low[0:112, :].bitcast(I32), in_=v_plane[4:116, :].bitcast(I32))
+
+        load_scales(w3_plane_raw, w3_scales)
+        nc.sync.dma_start(out=w1_raw[1][:], in_=w1_rows[1])
+
+        acc_warm = bank(7, "acc_warm")
+        for n in range(4):
+            nc.tensor.matmul_mx(
+                out=acc_warm[:],
+                lhsT=w2_raw[:, 0, 0:512].bitcast(FP8X4),
+                lhsT_scale=v_plane[:, 0:P],
+                rhs=w2_raw[:, 0, :].bitcast(FP8X4),
+                rhs_scale=v_plane[:, 0:HALF],
+                start=True,
+                stop=True,
+            )
 
         w2_codes = sb([P, PASSES, 4 * H], U8, "w2_codes")
         w2_plane = sb([P, PASSES, H], U8, "w2_plane")
         regroup(w2_codes, w2_raw)
         regroup(w2_plane, w2_plane_raw)
-
-        w3_raw = stage.tile([P, PASSES, 2 * H], U8, name="w3_raw", offset=12288 - 128)
-        nc.sync.dma_start(out=w3_raw[:].bitcast(I32), in_=w3_words.rearrange("a p b -> p a b").bitcast(I32))
-        w1_raw = [
-            stage.tile([P, PACK, H], F32, name=f"w1_raw{a}", offset=(0, 16384)[a]) for a in range(PASSES)
-        ]
-        for a in range(PASSES):
-            nc.sync.dma_start(
-                out=w1_raw[a][:], in_=w1[a * 512 : (a + 1) * 512, :].rearrange("(p j) c -> p j c", j=PACK)
-            )
-
-        v_plane = sb([P, S], U8, "v_plane")
-        picks = [offsets[:, s * HALF // 16 : (s + 1) * HALF // 16] for s in range(HALVES)]
-        for s in range(HALVES):
-            nc.vector.tensor_copy(v_plane[:, s * HALF : (s + 1) * HALF], tab_plane[:].indirect(picks[s]))
-        for r in range(4):
-            nc.scalar.dma_start(out=v_plane_low[r:P:32, :].bitcast(I32), in_=v_plane[4 + r : P : 32, :].bitcast(I32))
-        v_codes = [
-            [
-                stage.tile([P, HALF], U32, name=f"v_codes{a}_{s}", offset=24576 + 2048 * (2 * a + s), align_bytes=64)
-                for s in range(HALVES)
-            ]
-            for a in range(PASSES)
-        ]
+        v_codes = [[sb([P, HALF], U32, f"v_codes{a}_{s}") for s in range(HALVES)] for a in range(PASSES)]
         for a in range(PASSES):
             for s in range(HALVES):
                 nc.vector.tensor_copy(v_codes[a][s][:], tab[a][:].bitcast(U32).indirect(picks[s]))
@@ -124,10 +132,13 @@ def tile_list_pocket_max_affinity_kernel(
         regroup(w3_codes, w3_raw)
         regroup(w3_plane, w3_plane_raw)
 
-        wo_raw = stage.tile([P, PACK, N], F32, name="wo_raw", offset=12288 - 64)
+        wo_raw = stage.tile([P, PACK, N], F32, name="wo_raw", offset=0)
         wo_rows = wo.rearrange("(q t i) n -> t q i n", t=PACK, i=RUN)
         for t in range(PACK):
             nc.sync.dma_start(out=wo_raw[:, t, :], in_=wo_rows[t])
+        bo_col = stage.tile([P, N // P], F32, name="bo_col", offset=4 * KIB)
+        with nc.allow_non_contiguous_dma(reason="one bias value a partition"):
+            nc.sync.dma_start(out=bo_col[:], in_=bo.rearrange("(u p) -> p u", p=P))
 
         def product(acc, codes, plane, a, j0, width, low=False):
             s, c0 = divmod(j0, HALF)
@@ -144,7 +155,7 @@ def tile_list_pocket_max_affinity_kernel(
             )
 
         units = [(s, t) for s in range(HALVES) for t in range(PACK)]
-        acc_b = {u: psum.tile([P, HALF], F32, name="acc") for u in units}
+        acc_b = {u: bank(n, f"acc_b{n}") for n, u in enumerate(units)}
         for a in range(PASSES):
             for s, t in units:
                 product(
@@ -164,10 +175,10 @@ def tile_list_pocket_max_affinity_kernel(
         def cast_w1(a, t):
             src = w1_raw[a][:].rearrange("p j (q t i) -> p t q i j", t=PACK, i=RUN)[:, t]
             dst = w1_bf[a][:, t]
-            if a == 1 and t % 2 == 1:
-                nc.scalar.copy(out=dst.rearrange("p q i j -> p q j i"), in_=src.rearrange("p q i j -> p q j i"))
+            if a == 0:
+                nc.vector.tensor_copy(out=dst.rearrange("p q i j -> p q j i"), in_=src.rearrange("p q i j -> p q j i"))
             else:
-                nc.gpsimd.tensor_scalar(dst, src, 1.0, 0.0, MULT, ADD)
+                nc.scalar.copy(out=dst.rearrange("p q i j -> p q j i"), in_=src.rearrange("p q i j -> p q j i"))
 
         def quantize_w1(a):
             nc.vector.quantize_mx(
@@ -181,8 +192,8 @@ def tile_list_pocket_max_affinity_kernel(
                 cast_w1(a, t)
 
         bc_sb = {(s, t): sb([P, HALF], F32, f"bc_sb{s}_{t}") for s, t in units}
-        for s, t in units:
-            acc = psum.tile([P, HALF], F32, name="acc")
+        for n, (s, t) in enumerate(units):
+            acc = bank(n, f"acc_c{n}")
             for a in range(PASSES):
                 product(
                     acc,
@@ -193,39 +204,36 @@ def tile_list_pocket_max_affinity_kernel(
             nc.vector.scalar_tensor_tensor(
                 bc_sb[s, t][:], acc[:], bh_cols[t][:], b_sb[s, t][:], ADD, MAX
             )
-            if t == PACK - 1:
+            if n in (0, 6):
                 quantize_w1(s)
 
         wo_bf = sb([P, N, PACK], BF16, "wo_bf")
         wo_codes = sb([P, N], U32, "wo_codes")
         wo_plane = sb([P, N], U8, "wo_plane")
-        for u in range(N // P):
-            cols = slice(u * P, (u + 1) * P)
-            nc.gpsimd.tensor_scalar(
-                wo_bf[:, cols, :], wo_raw[:, :, cols].rearrange("p t n -> p n t"), 1.0, 0.0, MULT, ADD
-            )
-        nc.vector.quantize_mx(
-            out=wo_codes[:].bitcast(FP8X4), scales=wo_plane[:], in_=wo_bf[:].rearrange("p n t -> p (n t)")
+        nc.scalar.copy(
+            out=wo_bf[:].rearrange("p (c i) t -> p c t i", i=4), in_=wo_raw[:].rearrange("p t (c i) -> p c t i", i=4)
         )
 
         out_rows = out.rearrange("(u p) s -> p u s", p=P)
 
-        def second_product(h_rows, c0, j0):
-            h_bf = sb([P, PIECE, PACK], BF16, f"h_bf{j0}")
-            nc.scalar.copy(
+        def second_product(n, h_rows):
+            j0, width = PIECES[n]
+            h_bf = sb([P, width, PACK], BF16, f"h_bf{n}")
+            last = n == len(PIECES) - 1
+            (nc.vector.tensor_copy if last else nc.scalar.copy)(
                 out=h_bf[:].rearrange("p (c i) t -> p c t i", i=4),
-                in_=h_rows[:, :, c0 : c0 + PIECE].rearrange("p t (c i) -> p c t i", i=4),
+                in_=h_rows[:].rearrange("p t (c i) -> p c t i", i=4),
             )
-            h_codes = sb([P, PIECE], U32, f"h_codes{j0}")
-            h_plane = sb([P, PIECE], U8, f"h_plane{j0}")
+            h_codes = sb([P, width], U32, f"h_codes{n}")
+            h_plane = sb([P, width], U8, f"h_plane{n}")
             nc.vector.quantize_mx(
                 out=h_codes[:].bitcast(FP8X4), scales=h_plane[:], in_=h_bf[:].rearrange("p n t -> p (n t)")
             )
-            acc = psum.tile([P, HALF], F32, name="acc")
-            y = sb([P, N // P, PIECE], F32, f"y{j0}")
+            acc = bank(6 + n % 2, f"acc_y{n}")
+            y = sb([P, N // P, width], F32, f"y{n}")
             for u in range(N // P):
                 nc.tensor.matmul_mx(
-                    out=acc[:, u * PIECE : (u + 1) * PIECE],
+                    out=acc[:, u * width : (u + 1) * width],
                     lhsT=wo_codes[:, u * P : (u + 1) * P].bitcast(FP8X4),
                     lhsT_scale=wo_plane[:, u * P : (u + 1) * P],
                     rhs=h_codes[:].bitcast(FP8X4),
@@ -235,31 +243,35 @@ def tile_list_pocket_max_affinity_kernel(
                 )
             for u in range(N // P):
                 nc.scalar.activation(
-                    y[:, u, :], acc[:, u * PIECE : (u + 1) * PIECE], IDENT, bias=bo_col[:, u : u + 1]
+                    y[:, u, :], acc[:, u * width : (u + 1) * width], IDENT, bias=bo_col[:, u : u + 1]
                 )
-            nc.sync.dma_start(out=out_rows[:, :, j0 : j0 + PIECE], in_=y[:])
+            nc.sync.dma_start(out=out_rows[:, :, j0 : j0 + width], in_=y[:])
 
-        def third_pocket(j0):
+        def third_pocket(n):
+            j0, width = PIECES[n]
             s, c0 = divmod(j0, HALF)
-            h_rows = sb([P, PACK, PIECE], BF16, f"h_rows{j0}")
+            h_rows = sb([P, PACK, width], BF16, f"h_rows{n}")
             for t in range(PACK):
-                acc = psum.tile([P, HALF], F32, name="acc")
+                acc = bank((PACK * n + t) % 6, f"acc_a{n}_{t}")
                 for a in range(PASSES):
                     product(
                         acc,
                         w1_codes[a][:, t * P : (t + 1) * P].bitcast(FP8X4),
                         w1_plane[a][:, t * P : (t + 1) * P],
-                        a, j0, PIECE,
+                        a, j0, width,
                     )
                 nc.vector.scalar_tensor_tensor(
-                    h_rows[:, t, :], acc[:, :PIECE], bh_cols[t][:], bc_sb[s, t][:, c0 : c0 + PIECE], ADD, MAX
+                    h_rows[:, t, :], acc[:, :width], bh_cols[t][:], bc_sb[s, t][:, c0 : c0 + width], ADD, MAX
                 )
             return h_rows
 
-        starts = list(range(0, S, PIECE))
         rows = {}
-        for n in range(len(starts) + LAG):
-            if n < len(starts):
-                rows[n] = third_pocket(starts[n])
+        for n in range(len(PIECES) + LAG):
+            if n < len(PIECES):
+                rows[n] = third_pocket(n)
+            if n == 0:
+                nc.vector.quantize_mx(
+                    out=wo_codes[:].bitcast(FP8X4), scales=wo_plane[:], in_=wo_bf[:].rearrange("p n t -> p (n t)")
+                )
             if n >= LAG:
-                second_product(rows[n - LAG], 0, starts[n - LAG])
+                second_product(n - LAG, rows[n - LAG])

@@ -44,9 +44,9 @@ def tile_list_pocket_max_affinity_kernel(
         def bank(n, name):
             return psum.tile([P, HALF], F32, name=name, offset=2 * KIB * n)
 
-        def load_scales(plane, scales):
+        def load_scales(plane, scales, which):
             rows = scales.bitcast(I32).rearrange("a (g r) w -> r g a w", r=4)
-            for r in range(4):
+            for r in which:
                 nc.sync.dma_start(out=plane[r:P:32, :, :].bitcast(I32), in_=rows[r])
 
         def regroup(dst, src):
@@ -60,7 +60,7 @@ def tile_list_pocket_max_affinity_kernel(
         nc.sync.dma_start(offsets[:], offs)
 
         tab_plane = sb([P, T], U8, "tab_plane")
-        w2_plane_raw = sb([P, PASSES, H], U8, "w2_plane_raw")
+        w2_plane_raw = stage.tile([P, PASSES, H], U8, name="w2_plane_raw", offset=24 * KIB)
         w3_plane_raw = sb([P, PASSES, H], U8, "w3_plane_raw")
         v_plane_low = sb([P, S], U8, "v_plane_low")
         nc.gpsimd.memset(tab_plane[:].bitcast(I32), 0)
@@ -71,30 +71,32 @@ def tile_list_pocket_max_affinity_kernel(
         nc.vector.memset(warm[:, 0:8], 0.0)
         nc.scalar.activation(warm[:, 8:16], warm[:, 0:8], IDENT)
 
+        w2_raw = stage.tile([P, PASSES, 4 * H], U8, name="w2_raw", offset=16 * KIB)
+        nc.sync.dma_start(
+            out=w2_raw[:].bitcast(I32), in_=w2_words.rearrange("a p e i -> p a (e i)").bitcast(I32)
+        )
         for g in range(4):
             nc.sync.dma_start(
                 out=tab_plane[32 * g : 32 * g + 8, :].bitcast(I32),
                 in_=tab_scales.bitcast(I32)[:, 4 * g : 4 * g + 4, :],
             )
-        w2_raw = sb([P, PASSES, 4 * H], U8, "w2_raw")
-        nc.sync.dma_start(
-            out=w2_raw[:].bitcast(I32), in_=w2_words.rearrange("a p e i -> p a (e i)").bitcast(I32)
-        )
         tab_rows = tab_words.rearrange("a p t i -> a p (t i)").bitcast(I32)
         tab = [stage.tile([P, T], I32, name=f"tab{a}", offset=8 * KIB * a) for a in range(PASSES)]
-        load_scales(w2_plane_raw, w2_scales)
+        load_scales(w2_plane_raw, w2_scales, (0, 1))
         nc.sync.dma_start(out=tab[0][:], in_=tab_rows[0])
+        load_scales(w2_plane_raw, w2_scales, (2, 3))
         nc.sync.dma_start(out=tab[1][:], in_=tab_rows[1])
         w3_raw = sb([P, PASSES, 2 * H], U8, "w3_raw")
         nc.sync.dma_start(out=w3_raw[:].bitcast(I32), in_=w3_words.rearrange("a p b -> p a b").bitcast(I32))
+        load_scales(w3_plane_raw, w3_scales, range(4))
         bh_cols = [sb([P, 1], F32, f"bh_col{t}") for t in range(PACK)]
         with nc.allow_non_contiguous_dma(reason="one bias value a partition"):
             bh_rows = bh.rearrange("(q t i o) -> t q i o", t=PACK, i=RUN, o=1)
             for t in range(PACK):
-                nc.sync.dma_start(out=bh_cols[t][:], in_=bh_rows[t])
+                nc.gpsimd.dma_start(out=bh_cols[t][:], in_=bh_rows[t])
 
         w1_rows = w1.rearrange("(a p j) c -> a p j c", p=P, j=PACK)
-        w1_raw = [sb([P, PACK, H], F32, f"w1_raw{a}") for a in range(PASSES)]
+        w1_raw = [sb([P, PACK, H], F32, "w1_raw0")]
         nc.sync.dma_start(out=w1_raw[0][:], in_=w1_rows[0])
 
         picks = [offsets[:, s * HALF // 16 : (s + 1) * HALF // 16] for s in range(HALVES)]
@@ -103,8 +105,6 @@ def tile_list_pocket_max_affinity_kernel(
             nc.vector.tensor_copy(v_plane[:, s * HALF : (s + 1) * HALF], tab_plane[:].indirect(picks[s]))
         nc.scalar.dma_start(out=v_plane_low[0:112, :].bitcast(I32), in_=v_plane[4:116, :].bitcast(I32))
 
-        load_scales(w3_plane_raw, w3_scales)
-        nc.sync.dma_start(out=w1_raw[1][:], in_=w1_rows[1])
 
         acc_warm = bank(7, "acc_warm")
         for n in range(4):
@@ -121,11 +121,17 @@ def tile_list_pocket_max_affinity_kernel(
         w2_codes = sb([P, PASSES, 4 * H], U8, "w2_codes")
         w2_plane = sb([P, PASSES, H], U8, "w2_plane")
         regroup(w2_codes, w2_raw)
-        regroup(w2_plane, w2_plane_raw)
-        v_codes = [[sb([P, HALF], U32, f"v_codes{a}_{s}") for s in range(HALVES)] for a in range(PASSES)]
+        w1_raw.append(stage.tile([P, PACK, H], F32, name="w1_raw1", offset=16 * KIB))
+        nc.sync.dma_start(out=w1_raw[1][:], in_=w1_rows[1])
+        v_codes = {}
         for a in range(PASSES):
             for s in range(HALVES):
-                nc.vector.tensor_copy(v_codes[a][s][:], tab[a][:].bitcast(U32).indirect(picks[s]))
+                if (a, s) == (0, 1):
+                    regroup(w2_plane, w2_plane_raw)
+                    v_codes[a, s] = stage.tile([P, HALF], U32, name="v_codes0_1", offset=24 * KIB)
+                else:
+                    v_codes[a, s] = sb([P, HALF], U32, f"v_codes{a}_{s}")
+                nc.vector.tensor_copy(v_codes[a, s][:], tab[a][:].bitcast(U32).indirect(picks[s]))
 
         w3_codes = sb([P, PASSES, 2 * H], U8, "w3_codes")
         w3_plane = sb([P, PASSES, H], U8, "w3_plane")
@@ -148,7 +154,7 @@ def tile_list_pocket_max_affinity_kernel(
                 out=acc[:, :width],
                 lhsT=codes,
                 lhsT_scale=plane,
-                rhs=v_codes[a][s][:, c0 : c0 + width].bitcast(FP8X4),
+                rhs=v_codes[a, s][:, c0 : c0 + width].bitcast(FP8X4),
                 rhs_scale=scale,
                 start=(a == 0),
                 stop=(a == PASSES - 1),
@@ -219,7 +225,7 @@ def tile_list_pocket_max_affinity_kernel(
         def second_product(n, h_rows):
             j0, width = PIECES[n]
             h_bf = sb([P, width, PACK], BF16, f"h_bf{n}")
-            last = n == len(PIECES) - 1
+            last = n >= len(PIECES) - 2
             (nc.vector.tensor_copy if last else nc.scalar.copy)(
                 out=h_bf[:].rearrange("p (c i) t -> p c t i", i=4),
                 in_=h_rows[:].rearrange("p t (c i) -> p c t i", i=4),

@@ -1,6 +1,7 @@
 from contextlib import ExitStack
 
 import concourse.mybir as mybir
+from concourse.masks import make_identity
 
 K, T, S, H, N = 1024, 2048, 1024, 512, 256
 FLOPS = 2 * 3 * K * H * S + 2 * H * N * S
@@ -41,184 +42,205 @@ def tile_list_pocket_max_affinity_kernel(
         def sb(shape, dtype, name):
             return keep.tile(shape, dtype, name=name, align_bytes=64)
 
+        def staged(shape, dtype, name, kib):
+            return stage.tile(shape, dtype, name=name, offset=kib * KIB, align_bytes=64)
+
         def bank(n, name):
             return psum.tile([P, HALF], F32, name=name, offset=2 * KIB * n)
 
-        def load_scales(plane, scales, which):
+        def load_scales(plane, scales, which, queue=nc.sync):
             rows = scales.bitcast(I32).rearrange("a (g r) w -> r g a w", r=4)
             for r in which:
-                nc.sync.dma_start(out=plane[r:P:32, :, :].bitcast(I32), in_=rows[r])
+                queue.dma_start(out=plane[r:P:32, :, :].bitcast(I32), in_=rows[r])
 
         def regroup(dst, src):
-            for a in range(PASSES):
-                nc.vector.tensor_copy(
-                    out=dst[:, a, :].bitcast(I32).rearrange("p (t q w) -> p t q w", t=PACK, q=16),
-                    in_=src[:, a, :].bitcast(I32).rearrange("p (q t w) -> p t q w", t=PACK, q=16),
-                )
+            nc.vector.tensor_copy(
+                out=dst[:].bitcast(I32).rearrange("p a (t q w) -> p a t q w", t=PACK, q=16),
+                in_=src[:].bitcast(I32).rearrange("p a (q t w) -> p a t q w", t=PACK, q=16),
+            )
 
         offsets = keep.tile([P, S // 16], U16, name="offsets")
         nc.sync.dma_start(offsets[:], offs)
 
-        tab_plane = sb([P, T], U8, "tab_plane")
-        w2_plane_raw = stage.tile([P, PASSES, H], U8, name="w2_plane_raw", offset=24 * KIB)
+        tab_plane = staged([P, T], U8, "tab_plane", 28)
+        w2_plane_raw = staged([P, PASSES, H], U8, "w2_plane_raw", 26)
         w3_plane_raw = sb([P, PASSES, H], U8, "w3_plane_raw")
         v_plane_low = sb([P, S], U8, "v_plane_low")
-        nc.gpsimd.memset(tab_plane[:].bitcast(I32), 0)
+        nc.gpsimd.memset(tab_plane[:, 0 : T // 2].bitcast(I32), 0)
+        nc.vector.memset(tab_plane[:, T // 2 : T].bitcast(I32), 0)
         nc.gpsimd.memset(w2_plane_raw[:].bitcast(I32), 0)
+        bh_rows = sb([P, P], F32, "bh_rows")
+        nc.vector.memset(bh_rows[:], 0.0)
+        nc.scalar.dma_start(
+            out=bh_rows[0:PACK, :].rearrange("t (q i) -> t q i", i=RUN),
+            in_=bh.rearrange("(q t i) -> t q i", t=PACK, i=RUN),
+        )
+        identity = sb([P, P], F32, "identity")
+        make_identity(nc, identity[:])
         nc.vector.memset(w3_plane_raw[:].bitcast(I32), 0)
+        load_scales(w3_plane_raw, w3_scales, range(4), nc.gpsimd)
         nc.vector.memset(v_plane_low[:].bitcast(I32), 0)
+        bh_turned = bank(6, "bh_turned")
+        nc.tensor.transpose(bh_turned[:, 0:P], bh_rows[:], identity[:])
         warm = sb([P, 16], F32, "warm")
         nc.vector.memset(warm[:, 0:8], 0.0)
         nc.scalar.activation(warm[:, 8:16], warm[:, 0:8], IDENT)
 
-        w2_raw = stage.tile([P, PASSES, 4 * H], U8, name="w2_raw", offset=16 * KIB)
+        tab_scale_rows = tab_scales.bitcast(I32).rearrange("a (g r) w -> r g a w", r=4)
+        for r in range(4):
+            nc.sync.dma_start(out=tab_plane[r:P:16, :].bitcast(I32), in_=tab_scale_rows[r])
+        tab_rows = tab_words.rearrange("a p t i -> a p (t i)").bitcast(I32)
+        tab = [staged([P, T], I32, f"tab{a}", 8 * a) for a in range(PASSES)]
+        nc.sync.dma_start(out=tab[0][:], in_=tab_rows[0])
+        w2_raw = staged([P, PASSES, 4 * H], U8, "w2_raw", 16)
         nc.sync.dma_start(
             out=w2_raw[:].bitcast(I32), in_=w2_words.rearrange("a p e i -> p a (e i)").bitcast(I32)
         )
-        for g in range(4):
-            nc.sync.dma_start(
-                out=tab_plane[32 * g : 32 * g + 8, :].bitcast(I32),
-                in_=tab_scales.bitcast(I32)[:, 4 * g : 4 * g + 4, :],
-            )
-        tab_rows = tab_words.rearrange("a p t i -> a p (t i)").bitcast(I32)
-        tab = [stage.tile([P, T], I32, name=f"tab{a}", offset=8 * KIB * a) for a in range(PASSES)]
-        load_scales(w2_plane_raw, w2_scales, (0, 1))
-        nc.sync.dma_start(out=tab[0][:], in_=tab_rows[0])
-        load_scales(w2_plane_raw, w2_scales, (2, 3))
+        load_scales(w2_plane_raw, w2_scales, range(4))
         nc.sync.dma_start(out=tab[1][:], in_=tab_rows[1])
-        w3_raw = sb([P, PASSES, 2 * H], U8, "w3_raw")
+        w3_raw = staged([P, PASSES, 2 * H], U8, "w3_raw", 24)
         nc.sync.dma_start(out=w3_raw[:].bitcast(I32), in_=w3_words.rearrange("a p b -> p a b").bitcast(I32))
-        load_scales(w3_plane_raw, w3_scales, range(4))
-        bh_cols = [sb([P, 1], F32, f"bh_col{t}") for t in range(PACK)]
-        with nc.allow_non_contiguous_dma(reason="one bias value a partition"):
-            bh_rows = bh.rearrange("(q t i o) -> t q i o", t=PACK, i=RUN, o=1)
-            for t in range(PACK):
-                nc.gpsimd.dma_start(out=bh_cols[t][:], in_=bh_rows[t])
-
-        w1_rows = w1.rearrange("(a p j) c -> a p j c", p=P, j=PACK)
-        w1_raw = [sb([P, PACK, H], F32, "w1_raw0")]
-        nc.sync.dma_start(out=w1_raw[0][:], in_=w1_rows[0])
 
         picks = [offsets[:, s * HALF // 16 : (s + 1) * HALF // 16] for s in range(HALVES)]
         v_plane = sb([P, S], U8, "v_plane")
-        for s in range(HALVES):
-            nc.vector.tensor_copy(v_plane[:, s * HALF : (s + 1) * HALF], tab_plane[:].indirect(picks[s]))
-        nc.scalar.dma_start(out=v_plane_low[0:112, :].bitcast(I32), in_=v_plane[4:116, :].bitcast(I32))
-
+        nc.vector.tensor_copy(v_plane[:], tab_plane[:].indirect(offsets[:]))
+        nc.scalar.dma_start(out=v_plane_low[0:112, :].bitcast(I32), in_=v_plane[16:P, :].bitcast(I32))
+        v_planes = [v_plane, v_plane_low]
 
         acc_warm = bank(7, "acc_warm")
         for n in range(4):
             nc.tensor.matmul_mx(
                 out=acc_warm[:],
-                lhsT=w2_raw[:, 0, 0:512].bitcast(FP8X4),
-                lhsT_scale=v_plane[:, 0:P],
-                rhs=w2_raw[:, 0, :].bitcast(FP8X4),
-                rhs_scale=v_plane[:, 0:HALF],
+                lhsT=tab[0][:, 0:P].bitcast(FP8X4),
+                lhsT_scale=tab_plane[:, 0:P],
+                rhs=tab[0][:, 0:HALF].bitcast(FP8X4),
+                rhs_scale=tab_plane[:, 0:HALF],
                 start=True,
                 stop=True,
             )
 
+        bh_all = staged([P, PACK], F32, "bh_all", 28)
+        nc.scalar.activation(bh_all[:], bh_turned[:, 0:PACK], IDENT)
+        bh_cols = [bh_all[:, t : t + 1] for t in range(PACK)]
+
+        v_codes = {}
+
+        def gather_words(a, s, dst):
+            v_codes[a, s] = dst
+            nc.vector.tensor_copy(dst[:], tab[a][:].bitcast(U32).indirect(picks[s]))
+
+        gather_words(0, 0, sb([P, HALF], U32, "v_codes0_0"))
         w2_codes = sb([P, PASSES, 4 * H], U8, "w2_codes")
         w2_plane = sb([P, PASSES, H], U8, "w2_plane")
         regroup(w2_codes, w2_raw)
-        w1_raw.append(stage.tile([P, PACK, H], F32, name="w1_raw1", offset=16 * KIB))
+        regroup(w2_plane, w2_plane_raw)
+
+        w1_rows = w1.rearrange("(a p j) c -> a p j c", p=P, j=PACK)
+        w1_raw = [staged([P, PACK, H], F32, "w1_raw0", 16)]
+        nc.sync.dma_start(out=w1_raw[0][:], in_=w1_rows[0])
+
+        gather_words(0, 1, staged([P, HALF], U32, "v_codes0_1", 26))
+        w1_raw.append(staged([P, PACK, H], F32, "w1_raw1", 0))
         nc.sync.dma_start(out=w1_raw[1][:], in_=w1_rows[1])
-        v_codes = {}
-        for a in range(PASSES):
-            for s in range(HALVES):
-                if (a, s) == (0, 1):
-                    regroup(w2_plane, w2_plane_raw)
-                    v_codes[a, s] = stage.tile([P, HALF], U32, name="v_codes0_1", offset=24 * KIB)
-                else:
-                    v_codes[a, s] = sb([P, HALF], U32, f"v_codes{a}_{s}")
-                nc.vector.tensor_copy(v_codes[a, s][:], tab[a][:].bitcast(U32).indirect(picks[s]))
+        gather_words(1, 0, sb([P, HALF], U32, "v_codes1_0"))
 
         w3_codes = sb([P, PASSES, 2 * H], U8, "w3_codes")
         w3_plane = sb([P, PASSES, H], U8, "w3_plane")
-        regroup(w3_codes, w3_raw)
         regroup(w3_plane, w3_plane_raw)
+        regroup(w3_codes, w3_raw)
+        gather_words(1, 1, staged([P, HALF], U32, "v_codes1_1", 24))
 
-        wo_raw = stage.tile([P, PACK, N], F32, name="wo_raw", offset=0)
+        wo_raw = staged([P, PACK, N], F32, "wo_raw", 8)
         wo_rows = wo.rearrange("(q t i) n -> t q i n", t=PACK, i=RUN)
         for t in range(PACK):
             nc.sync.dma_start(out=wo_raw[:, t, :], in_=wo_rows[t])
-        bo_col = stage.tile([P, N // P], F32, name="bo_col", offset=4 * KIB)
+        bo_col = staged([P, N // P], F32, "bo_col", 12)
         with nc.allow_non_contiguous_dma(reason="one bias value a partition"):
             nc.sync.dma_start(out=bo_col[:], in_=bo.rearrange("(u p) -> p u", p=P))
 
-        def product(acc, codes, plane, a, j0, width, low=False):
+        def product(acc, codes, plane, a, j0, width):
             s, c0 = divmod(j0, HALF)
-            cols = slice(j0, j0 + width)
-            scale = v_plane_low[:, cols] if low and a == 1 else v_plane[4 * a : P, cols]
             nc.tensor.matmul_mx(
                 out=acc[:, :width],
                 lhsT=codes,
                 lhsT_scale=plane,
                 rhs=v_codes[a, s][:, c0 : c0 + width].bitcast(FP8X4),
-                rhs_scale=scale,
+                rhs_scale=v_planes[a][:, j0 : j0 + width],
                 start=(a == 0),
                 stop=(a == PASSES - 1),
             )
 
         units = [(s, t) for s in range(HALVES) for t in range(PACK)]
         acc_b = {u: bank(n, f"acc_b{n}") for n, u in enumerate(units)}
-        for a in range(PASSES):
-            for s, t in units:
-                product(
-                    acc_b[s, t],
-                    w2_codes[:, a, t * 512 : (t + 1) * 512].bitcast(FP8X4),
-                    w2_plane[:, a, t * P : (t + 1) * P],
-                    a, s * HALF, HALF,
-                )
         b_sb = {(s, t): sb([P, HALF], F32, f"b_sb{s}_{t}") for s, t in units}
-        for s, t in units:
-            nc.scalar.activation(b_sb[s, t][:], acc_b[s, t][:], IDENT, bias=bh_cols[t][:])
-
-        w1_bf = [sb([P, PACK, 16, RUN, PACK], BF16, f"w1_bf{a}") for a in range(PASSES)]
-        w1_codes = [sb([P, H], U32, f"w1_codes{a}") for a in range(PASSES)]
-        w1_plane = [sb([P, H], U8, f"w1_plane{a}") for a in range(PASSES)]
-
-        def cast_w1(a, t):
-            src = w1_raw[a][:].rearrange("p j (q t i) -> p t q i j", t=PACK, i=RUN)[:, t]
-            dst = w1_bf[a][:, t]
-            if a == 0:
-                nc.vector.tensor_copy(out=dst.rearrange("p q i j -> p q j i"), in_=src.rearrange("p q i j -> p q j i"))
-            else:
-                nc.scalar.copy(out=dst.rearrange("p q i j -> p q j i"), in_=src.rearrange("p q i j -> p q j i"))
-
-        def quantize_w1(a):
-            nc.vector.quantize_mx(
-                out=w1_codes[a][:].bitcast(FP8X4),
-                scales=w1_plane[a][:],
-                in_=w1_bf[a][:].rearrange("p t q i j -> p (t q i j)"),
-            )
-
-        for a in range(PASSES):
-            for t in range(PACK):
-                cast_w1(a, t)
-
         bc_sb = {(s, t): sb([P, HALF], F32, f"bc_sb{s}_{t}") for s, t in units}
-        for n, (s, t) in enumerate(units):
-            acc = bank(n, f"acc_c{n}")
+
+        def b_pass(a, s, t):
+            product(
+                acc_b[s, t],
+                w2_codes[:, a, t * 512 : (t + 1) * 512].bitcast(FP8X4),
+                w2_plane[:, a, t * P : (t + 1) * P],
+                a, s * HALF, HALF,
+            )
+            if a == PASSES - 1:
+                nc.scalar.activation(b_sb[s, t][:], acc_b[s, t][:], IDENT, bias=bh_cols[t])
+
+        def c_unit(s, t):
+            acc = bank(PACK * s + t, f"acc_c{s}_{t}")
             for a in range(PASSES):
                 product(
                     acc,
                     w3_codes[:, a, t * 256 : (t + 1) * 256].bitcast(FP4X4),
                     w3_plane[:, a, t * P : (t + 1) * P],
-                    a, s * HALF, HALF, low=True,
+                    a, s * HALF, HALF,
                 )
             nc.vector.scalar_tensor_tensor(
-                bc_sb[s, t][:], acc[:], bh_cols[t][:], b_sb[s, t][:], ADD, MAX
+                bc_sb[s, t][:], acc[:], bh_cols[t], b_sb[s, t][:], ADD, MAX
             )
-            if n in (0, 6):
-                quantize_w1(s)
 
+        w1_bf = [sb([P, PACK, 16, RUN, PACK], BF16, f"w1_bf{a}") for a in range(PASSES)]
+        w1_codes = [sb([P, H], U32, f"w1_codes{a}") for a in range(PASSES)]
+        w1_plane = [sb([P, H], U8, f"w1_plane{a}") for a in range(PASSES)]
+
+        def cast_w1(a, t, on_gpsimd):
+            src = w1_raw[a][:].rearrange("p j (q t i) -> p t q i j", t=PACK, i=RUN)[:, t]
+            dst = w1_bf[a][:, t]
+            if on_gpsimd:
+                nc.gpsimd.tensor_scalar(out=dst, in0=src, scalar1=1.0, scalar2=0.0, op0=MULT, op1=ADD)
+            else:
+                nc.scalar.copy(out=dst.rearrange("p q i j -> p q j i"), in_=src.rearrange("p q i j -> p q j i"))
+
+        def quantize_w1(a, t0, t1):
+            nc.vector.quantize_mx(
+                out=w1_codes[a][:, t0 * P : t1 * P].bitcast(FP8X4),
+                scales=w1_plane[a][:, t0 * P : t1 * P],
+                in_=w1_bf[a][:, t0:t1].rearrange("p t q i j -> p (t q i j)"),
+            )
+
+        for s, t in units:
+            b_pass(0, s, t)
+        for t in range(PACK):
+            b_pass(1, 0, t)
+        for t in range(PACK):
+            c_unit(0, t)
+            b_pass(1, 1, t)
+        for t in range(PACK):
+            cast_w1(0, t, t < 3)
+        for t in range(PACK):
+            cast_w1(1, t, t >= 2)
         wo_bf = sb([P, N, PACK], BF16, "wo_bf")
         wo_codes = sb([P, N], U32, "wo_codes")
         wo_plane = sb([P, N], U8, "wo_plane")
-        nc.scalar.copy(
-            out=wo_bf[:].rearrange("p (c i) t -> p c t i", i=4), in_=wo_raw[:].rearrange("p t (c i) -> p c t i", i=4)
+        nc.gpsimd.tensor_scalar(
+            out=wo_bf[:], in0=wo_raw[:].rearrange("p t n -> p n t"), scalar1=1.0, scalar2=0.0, op0=MULT, op1=ADD
         )
+        c_unit(1, 0)
+        quantize_w1(0, 0, 4)
+        c_unit(1, 1)
+        c_unit(1, 2)
+        quantize_w1(1, 0, 2)
+        c_unit(1, 3)
+        quantize_w1(1, 2, 4)
 
         out_rows = out.rearrange("(u p) s -> p u s", p=P)
 
@@ -267,7 +289,7 @@ def tile_list_pocket_max_affinity_kernel(
                         a, j0, width,
                     )
                 nc.vector.scalar_tensor_tensor(
-                    h_rows[:, t, :], acc[:, :width], bh_cols[t][:], bc_sb[s, t][:, c0 : c0 + width], ADD, MAX
+                    h_rows[:, t, :], acc[:, :width], bh_cols[t], bc_sb[s, t][:, c0 : c0 + width], ADD, MAX
                 )
             return h_rows
 

@@ -208,7 +208,8 @@ def tile_list_pocket_max_affinity_kernel(
             if on_gpsimd:
                 nc.gpsimd.tensor_scalar(out=dst, in0=src, scalar1=1.0, scalar2=0.0, op0=MULT, op1=ADD)
             else:
-                nc.scalar.copy(out=dst.rearrange("p q i j -> p q j i"), in_=src.rearrange("p q i j -> p q j i"))
+                order = "p q (h i) j -> p q h j i"
+                nc.scalar.copy(out=dst.rearrange(order, h=2), in_=src.rearrange(order, h=2))
 
         def quantize_w1(a, t0, t1):
             nc.vector.quantize_mx(

@@ -28,6 +28,7 @@ HALVES = S // HALF
 LAG = 1
 PIECES = [(0, 256), (256, 256), (512, 256), (768, 128), (896, 128)]
 KIB = 1024
+Y_LAST = [(4, 5), (2, 3)]
 
 
 def tile_list_pocket_max_affinity_kernel(
@@ -62,26 +63,19 @@ def tile_list_pocket_max_affinity_kernel(
         offsets = keep.tile([P, S // 16], U16, name="offsets")
         nc.sync.dma_start(offsets[:], offs)
 
-        tab_plane = staged([P, T], U8, "tab_plane", 28)
-        w2_plane_raw = staged([P, PASSES, H], U8, "w2_plane_raw", 26)
-        w3_plane_raw = sb([P, PASSES, H], U8, "w3_plane_raw")
+        tab_plane = sb([P, T], U8, "tab_plane")
+        w2_plane_raw = staged([P, PASSES, H], U8, "w2_plane_raw", 16)
+        w3_plane_raw = staged([P, PASSES, H], U8, "w3_plane_raw", 18)
         v_plane_low = sb([P, S], U8, "v_plane_low")
         nc.gpsimd.memset(tab_plane[:, 0 : T // 2].bitcast(I32), 0)
         nc.vector.memset(tab_plane[:, T // 2 : T].bitcast(I32), 0)
-        nc.gpsimd.memset(w2_plane_raw[:].bitcast(I32), 0)
         bh_rows = sb([P, P], F32, "bh_rows")
         nc.vector.memset(bh_rows[:], 0.0)
-        nc.scalar.dma_start(
-            out=bh_rows[0:PACK, :].rearrange("t (q i) -> t q i", i=RUN),
-            in_=bh.rearrange("(q t i) -> t q i", t=PACK, i=RUN),
-        )
+        nc.vector.memset(w2_plane_raw[:].bitcast(I32), 0)
+        nc.vector.memset(w3_plane_raw[:].bitcast(I32), 0)
+        nc.vector.memset(v_plane_low[:].bitcast(I32), 0)
         identity = sb([P, P], F32, "identity")
         make_identity(nc, identity[:])
-        nc.vector.memset(w3_plane_raw[:].bitcast(I32), 0)
-        load_scales(w3_plane_raw, w3_scales, range(4), nc.gpsimd)
-        nc.vector.memset(v_plane_low[:].bitcast(I32), 0)
-        bh_turned = bank(6, "bh_turned")
-        nc.tensor.transpose(bh_turned[:, 0:P], bh_rows[:], identity[:])
         warm = sb([P, 16], F32, "warm")
         nc.vector.memset(warm[:, 0:8], 0.0)
         nc.scalar.activation(warm[:, 8:16], warm[:, 0:8], IDENT)
@@ -92,22 +86,39 @@ def tile_list_pocket_max_affinity_kernel(
         tab_rows = tab_words.rearrange("a p t i -> a p (t i)").bitcast(I32)
         tab = [staged([P, T], I32, f"tab{a}", 8 * a) for a in range(PASSES)]
         nc.sync.dma_start(out=tab[0][:], in_=tab_rows[0])
-        w2_raw = staged([P, PASSES, 4 * H], U8, "w2_raw", 16)
+        w2_raw = sb([P, PASSES, 4 * H], U8, "w2_raw")
         nc.sync.dma_start(
             out=w2_raw[:].bitcast(I32), in_=w2_words.rearrange("a p e i -> p a (e i)").bitcast(I32)
         )
+        nc.sync.dma_start(
+            out=bh_rows[0:PACK, :].rearrange("t (q i) -> t q i", i=RUN),
+            in_=bh.rearrange("(q t i) -> t q i", t=PACK, i=RUN),
+        )
         load_scales(w2_plane_raw, w2_scales, range(4))
         nc.sync.dma_start(out=tab[1][:], in_=tab_rows[1])
-        w3_raw = staged([P, PASSES, 2 * H], U8, "w3_raw", 24)
+        w3_raw = sb([P, PASSES, 2 * H], U8, "w3_raw")
         nc.sync.dma_start(out=w3_raw[:].bitcast(I32), in_=w3_words.rearrange("a p b -> p a b").bitcast(I32))
 
         picks = [offsets[:, s * HALF // 16 : (s + 1) * HALF // 16] for s in range(HALVES)]
         v_plane = sb([P, S], U8, "v_plane")
         nc.vector.tensor_copy(v_plane[:], tab_plane[:].indirect(offsets[:]))
-        nc.scalar.dma_start(out=v_plane_low[0:112, :].bitcast(I32), in_=v_plane[16:P, :].bitcast(I32))
+        nc.sync.dma_start(out=v_plane_low[0:112, :].bitcast(I32), in_=v_plane[16:P, :].bitcast(I32))
         v_planes = [v_plane, v_plane_low]
+        load_scales(w3_plane_raw, w3_scales, range(4))
 
-        acc_warm = bank(7, "acc_warm")
+        w1_rows = w1.rearrange("(a p j) c -> a p j c", p=P, j=PACK)
+        w1_raw = [sb([P, PACK, H], F32, "w1_raw0"), staged([P, PACK, H], F32, "w1_raw1", 20)]
+        for a in range(PASSES):
+            nc.sync.dma_start(out=w1_raw[a][:], in_=w1_rows[a])
+        wo_raw = sb([P, PACK, N], F32, "wo_raw")
+        wo_rows = wo.rearrange("(q t i) n -> t q i n", t=PACK, i=RUN)
+        for t in range(PACK):
+            nc.sync.dma_start(out=wo_raw[:, t, :], in_=wo_rows[t])
+        bo_col = sb([P, N // P], F32, "bo_col")
+        with nc.allow_non_contiguous_dma(reason="one bias value a partition"):
+            nc.sync.dma_start(out=bo_col[:], in_=bo.rearrange("(u p) -> p u", p=P))
+
+        acc_warm = bank(6, "acc_warm")
         for n in range(4):
             nc.tensor.matmul_mx(
                 out=acc_warm[:],
@@ -119,7 +130,9 @@ def tile_list_pocket_max_affinity_kernel(
                 stop=True,
             )
 
-        bh_all = staged([P, PACK], F32, "bh_all", 28)
+        bh_turned = bank(7, "bh_turned")
+        nc.tensor.transpose(bh_turned[:, 0:P], bh_rows[:], identity[:])
+        bh_all = sb([P, PACK], F32, "bh_all")
         nc.scalar.activation(bh_all[:], bh_turned[:, 0:PACK], IDENT)
         bh_cols = [bh_all[:, t : t + 1] for t in range(PACK)]
 
@@ -134,29 +147,13 @@ def tile_list_pocket_max_affinity_kernel(
         w2_plane = sb([P, PASSES, H], U8, "w2_plane")
         regroup(w2_codes, w2_raw)
         regroup(w2_plane, w2_plane_raw)
-
-        w1_rows = w1.rearrange("(a p j) c -> a p j c", p=P, j=PACK)
-        w1_raw = [staged([P, PACK, H], F32, "w1_raw0", 16)]
-        nc.sync.dma_start(out=w1_raw[0][:], in_=w1_rows[0])
-
-        gather_words(0, 1, staged([P, HALF], U32, "v_codes0_1", 26))
-        w1_raw.append(staged([P, PACK, H], F32, "w1_raw1", 0))
-        nc.sync.dma_start(out=w1_raw[1][:], in_=w1_rows[1])
+        gather_words(0, 1, staged([P, HALF], U32, "v_codes0_1", 16))
         gather_words(1, 0, sb([P, HALF], U32, "v_codes1_0"))
-
         w3_codes = sb([P, PASSES, 2 * H], U8, "w3_codes")
         w3_plane = sb([P, PASSES, H], U8, "w3_plane")
-        regroup(w3_plane, w3_plane_raw)
         regroup(w3_codes, w3_raw)
-        gather_words(1, 1, staged([P, HALF], U32, "v_codes1_1", 24))
-
-        wo_raw = staged([P, PACK, N], F32, "wo_raw", 8)
-        wo_rows = wo.rearrange("(q t i) n -> t q i n", t=PACK, i=RUN)
-        for t in range(PACK):
-            nc.sync.dma_start(out=wo_raw[:, t, :], in_=wo_rows[t])
-        bo_col = staged([P, N // P], F32, "bo_col", 12)
-        with nc.allow_non_contiguous_dma(reason="one bias value a partition"):
-            nc.sync.dma_start(out=bo_col[:], in_=bo.rearrange("(u p) -> p u", p=P))
+        regroup(w3_plane, w3_plane_raw)
+        gather_words(1, 1, staged([P, HALF], U32, "v_codes1_1", 18))
 
         def product(acc, codes, plane, a, j0, width):
             s, c0 = divmod(j0, HALF)
@@ -170,41 +167,46 @@ def tile_list_pocket_max_affinity_kernel(
                 stop=(a == PASSES - 1),
             )
 
-        units = [(s, t) for s in range(HALVES) for t in range(PACK)]
-        acc_b = {u: bank(n, f"acc_b{n}") for n, u in enumerate(units)}
-        b_sb = {(s, t): sb([P, HALF], F32, f"b_sb{s}_{t}") for s, t in units}
-        bc_sb = {(s, t): sb([P, HALF], F32, f"bc_sb{s}_{t}") for s, t in units}
+        acc_b, acc_c, b_sb, bc_sb = {}, {}, {}, {}
 
         def b_pass(a, s, t):
+            if a == 0:
+                acc_b[s, t] = bank(PACK * s + t, f"acc_b{s}_{t}")
             product(
                 acc_b[s, t],
                 w2_codes[:, a, t * 512 : (t + 1) * 512].bitcast(FP8X4),
                 w2_plane[:, a, t * P : (t + 1) * P],
                 a, s * HALF, HALF,
             )
-            if a == PASSES - 1:
-                nc.scalar.activation(b_sb[s, t][:], acc_b[s, t][:], IDENT, bias=bh_cols[t])
 
-        def c_unit(s, t):
-            acc = bank(PACK * s + t, f"acc_c{s}_{t}")
-            for a in range(PASSES):
-                product(
-                    acc,
-                    w3_codes[:, a, t * 256 : (t + 1) * 256].bitcast(FP4X4),
-                    w3_plane[:, a, t * P : (t + 1) * P],
-                    a, s * HALF, HALF,
-                )
-            nc.vector.scalar_tensor_tensor(
-                bc_sb[s, t][:], acc[:], bh_cols[t], b_sb[s, t][:], ADD, MAX
+        def b_out(s, t, dst):
+            b_sb[s, t] = dst
+            nc.scalar.activation(dst[:], acc_b[s, t][:], IDENT, bias=bh_cols[t])
+
+        def c_pass(a, s, t):
+            if a == 0:
+                acc_c[s, t] = bank(PACK * s + t, f"acc_c{s}_{t}")
+            product(
+                acc_c[s, t],
+                w3_codes[:, a, t * 256 : (t + 1) * 256].bitcast(FP4X4),
+                w3_plane[:, a, t * P : (t + 1) * P],
+                a, s * HALF, HALF,
             )
 
-        w1_bf = [sb([P, PACK, 16, RUN, PACK], BF16, f"w1_bf{a}") for a in range(PASSES)]
+        def c_out(s, t, dst):
+            bc_sb[s, t] = dst
+            nc.vector.scalar_tensor_tensor(dst[:], acc_c[s, t][:], bh_cols[t], b_sb[s, t][:], ADD, MAX)
+
+        w1_bf = {
+            (0, 0): staged([P, 4, 16, RUN, PACK], BF16, "w1_bf0_0", 28),
+            (1, 0): staged([P, 4, 16, RUN, PACK], BF16, "w1_bf1_0", 32),
+        }
         w1_codes = [sb([P, H], U32, f"w1_codes{a}") for a in range(PASSES)]
         w1_plane = [sb([P, H], U8, f"w1_plane{a}") for a in range(PASSES)]
 
-        def cast_w1(a, t, on_gpsimd):
+        def cast_w1(a, t0, t, on_gpsimd):
             src = w1_raw[a][:].rearrange("p j (q t i) -> p t q i j", t=PACK, i=RUN)[:, t]
-            dst = w1_bf[a][:, t]
+            dst = w1_bf[a, t0][:, t - t0]
             if on_gpsimd:
                 nc.gpsimd.tensor_scalar(out=dst, in0=src, scalar1=1.0, scalar2=0.0, op0=MULT, op1=ADD)
             else:
@@ -215,33 +217,52 @@ def tile_list_pocket_max_affinity_kernel(
             nc.vector.quantize_mx(
                 out=w1_codes[a][:, t0 * P : t1 * P].bitcast(FP8X4),
                 scales=w1_plane[a][:, t0 * P : t1 * P],
-                in_=w1_bf[a][:, t0:t1].rearrange("p t q i j -> p (t q i j)"),
+                in_=w1_bf[a, t0][:].rearrange("p t q i j -> p (t q i j)"),
             )
 
-        for s, t in units:
-            b_pass(0, s, t)
+        def whole(one_pass, s, t):
+            for a in range(PASSES):
+                one_pass(a, s, t)
+
+        def c_unit(s, t, dst):
+            whole(c_pass, s, t)
+            c_out(s, t, dst)
+
+        def b_end(s, t, dst):
+            b_pass(1, s, t)
+            b_out(s, t, dst)
+
+        for s in range(HALVES):
+            for t in range(PACK):
+                b_pass(0, s, t)
         for t in range(PACK):
-            b_pass(1, 0, t)
+            b_end(0, t, sb([P, HALF], F32, f"b_sb0_{t}"))
+        c_unit(0, 0, sb([P, HALF], F32, "bc_sb0_0"))
+        c_unit(0, 1, sb([P, HALF], F32, "bc_sb0_1"))
+        b_end(1, 0, sb([P, HALF], F32, "b_sb1_0"))
+        c_unit(0, 2, sb([P, HALF], F32, "bc_sb0_2"))
+        b_end(1, 1, sb([P, HALF], F32, "b_sb1_1"))
+        c_unit(0, 3, sb([P, HALF], F32, "bc_sb0_3"))
+        b_end(1, 2, sb([P, HALF], F32, "b_sb1_2"))
+        b_end(1, 3, sb([P, HALF], F32, "b_sb1_3"))
         for t in range(PACK):
-            c_unit(0, t)
-            b_pass(1, 1, t)
+            cast_w1(0, 0, t, True)
         for t in range(PACK):
-            cast_w1(0, t, t < 3)
-        for t in range(PACK):
-            cast_w1(1, t, t >= 2)
+            cast_w1(1, 0, t, t < 2)
+        c_unit(1, 0, sb([P, HALF], F32, "bc_sb1_0"))
+        quantize_w1(0, 0, 4)
+        c_unit(1, 1, staged([P, HALF], F32, "bc_sb1_1", 28))
+        c_unit(1, 2, staged([P, HALF], F32, "bc_sb1_2", 30))
+        quantize_w1(1, 0, 4)
+        c_unit(1, 3, staged([P, HALF], F32, "bc_sb1_3", 32))
+
         wo_bf = sb([P, N, PACK], BF16, "wo_bf")
         wo_codes = sb([P, N], U32, "wo_codes")
         wo_plane = sb([P, N], U8, "wo_plane")
-        nc.gpsimd.tensor_scalar(
-            out=wo_bf[:], in0=wo_raw[:].rearrange("p t n -> p n t"), scalar1=1.0, scalar2=0.0, op0=MULT, op1=ADD
+        nc.scalar.copy(
+            out=wo_bf[:].rearrange("p (c i) t -> p c t i", i=4),
+            in_=wo_raw[:].rearrange("p t (c i) -> p c t i", i=4),
         )
-        c_unit(1, 0)
-        quantize_w1(0, 0, 4)
-        c_unit(1, 1)
-        c_unit(1, 2)
-        quantize_w1(1, 0, 2)
-        c_unit(1, 3)
-        quantize_w1(1, 2, 4)
 
         out_rows = out.rearrange("(u p) s -> p u s", p=P)
 
@@ -258,11 +279,17 @@ def tile_list_pocket_max_affinity_kernel(
             nc.vector.quantize_mx(
                 out=h_codes[:].bitcast(FP8X4), scales=h_plane[:], in_=h_bf[:].rearrange("p n t -> p (n t)")
             )
-            acc = bank(6 + n % 2, f"acc_y{n}")
             y = sb([P, N // P, width], F32, f"y{n}")
+            accs = []
             for u in range(N // P):
+                if last:
+                    accs.append(bank(Y_LAST[n % 2][u], f"acc_y{n}_{u}")[:, 0:width])
+                else:
+                    if u == 0:
+                        both = bank(6 + n % 2, f"acc_y{n}")
+                    accs.append(both[:, u * width : (u + 1) * width])
                 nc.tensor.matmul_mx(
-                    out=acc[:, u * width : (u + 1) * width],
+                    out=accs[u],
                     lhsT=wo_codes[:, u * P : (u + 1) * P].bitcast(FP8X4),
                     lhsT_scale=wo_plane[:, u * P : (u + 1) * P],
                     rhs=h_codes[:].bitcast(FP8X4),
@@ -271,9 +298,10 @@ def tile_list_pocket_max_affinity_kernel(
                     stop=True,
                 )
             for u in range(N // P):
-                nc.scalar.activation(
-                    y[:, u, :], acc[:, u * width : (u + 1) * width], IDENT, bias=bo_col[:, u : u + 1]
-                )
+                if last and u == 1:
+                    nc.vector.tensor_scalar_add(y[:, u, :], accs[u], bo_col[:, u : u + 1])
+                else:
+                    nc.scalar.activation(y[:, u, :], accs[u], IDENT, bias=bo_col[:, u : u + 1])
             nc.sync.dma_start(out=out_rows[:, :, j0 : j0 + width], in_=y[:])
 
         def third_pocket(n):

@@ -270,7 +270,8 @@ def tile_list_pocket_max_affinity_kernel(
             j0, width = PIECES[n]
             h_bf = sb([P, width, PACK], BF16, f"h_bf{n}")
             last = n >= len(PIECES) - 2
-            (nc.vector.tensor_copy if last else nc.scalar.copy)(
+            final = n == len(PIECES) - 1
+            (nc.vector.tensor_copy if final else nc.scalar.copy)(
                 out=h_bf[:].rearrange("p (c i) t -> p c t i", i=4),
                 in_=h_rows[:].rearrange("p t (c i) -> p c t i", i=4),
             )
@@ -298,7 +299,7 @@ def tile_list_pocket_max_affinity_kernel(
                     stop=True,
                 )
             for u in range(N // P):
-                if last and u == 1:
+                if final and u == 1:
                     nc.vector.tensor_scalar_add(y[:, u, :], accs[u], bo_col[:, u : u + 1])
                 else:
                     nc.scalar.activation(y[:, u, :], accs[u], IDENT, bias=bo_col[:, u : u + 1])

@@ -256,12 +256,11 @@ def tile_list_pocket_max_affinity_kernel(
         quantize_w1(1, 0, 4)
         c_unit(1, 3, staged([P, HALF], F32, "bc_sb1_3", 32))
 
-        wo_bf = sb([P, N, PACK], BF16, "wo_bf")
+        wo_bf = staged([P, N, PACK], BF16, "wo_bf", 34)
         wo_codes = sb([P, N], U32, "wo_codes")
         wo_plane = sb([P, N], U8, "wo_plane")
-        nc.scalar.copy(
-            out=wo_bf[:].rearrange("p (c i) t -> p c t i", i=4),
-            in_=wo_raw[:].rearrange("p t (c i) -> p c t i", i=4),
+        nc.gpsimd.tensor_scalar(
+            out=wo_bf[:], in0=wo_raw[:].rearrange("p t n -> p n t"), scalar1=1.0, scalar2=0.0, op0=MULT, op1=ADD
         )
 
         out_rows = out.rearrange("(u p) s -> p u s", p=P)

@@ -28,7 +28,9 @@ HALVES = S // HALF
 LAG = 1
 PIECES = [(0, 256), (256, 256), (512, 256), (768, 128), (896, 128)]
 KIB = 1024
-Y_LAST = [(4, 5), (2, 3)]
+A_BANKS = [4, 5, 0, 1, 2, 3]
+Y_LAST = [(2, 3), (0, 1)]
+EDGE = 1 / 16
 
 
 def tile_list_pocket_max_affinity_kernel(
@@ -44,7 +46,7 @@ def tile_list_pocket_max_affinity_kernel(
             return keep.tile(shape, dtype, name=name, align_bytes=64)
 
         def staged(shape, dtype, name, kib):
-            return stage.tile(shape, dtype, name=name, offset=kib * KIB, align_bytes=64)
+            return stage.tile(shape, dtype, name=name, offset=int(kib * KIB), align_bytes=64)
 
         def bank(n, name):
             return psum.tile([P, HALF], F32, name=name, offset=2 * KIB * n)
@@ -107,7 +109,7 @@ def tile_list_pocket_max_affinity_kernel(
         load_scales(w3_plane_raw, w3_scales, range(4))
 
         w1_rows = w1.rearrange("(a p j) c -> a p j c", p=P, j=PACK)
-        w1_raw = [sb([P, PACK, H], F32, "w1_raw0"), staged([P, PACK, H], F32, "w1_raw1", 20)]
+        w1_raw = [staged([P, PACK, H], F32, "w1_raw0", 28), staged([P, PACK, H], F32, "w1_raw1", 20)]
         for a in range(PASSES):
             nc.sync.dma_start(out=w1_raw[a][:], in_=w1_rows[a])
         wo_raw = sb([P, PACK, N], F32, "wo_raw")
@@ -185,7 +187,7 @@ def tile_list_pocket_max_affinity_kernel(
 
         def c_pass(a, s, t):
             if a == 0:
-                acc_c[s, t] = bank(PACK * s + t, f"acc_c{s}_{t}")
+                acc_c[s, t] = bank(t, f"acc_c{s}_{t}")
             product(
                 acc_c[s, t],
                 w3_codes[:, a, t * 256 : (t + 1) * 256].bitcast(FP4X4),
@@ -198,8 +200,8 @@ def tile_list_pocket_max_affinity_kernel(
             nc.vector.scalar_tensor_tensor(dst[:], acc_c[s, t][:], bh_cols[t], b_sb[s, t][:], ADD, MAX)
 
         w1_bf = {
-            (0, 0): staged([P, 4, 16, RUN, PACK], BF16, "w1_bf0_0", 28),
-            (1, 0): staged([P, 4, 16, RUN, PACK], BF16, "w1_bf1_0", 32),
+            (0, 0): staged([P, 4, 16, RUN, PACK], BF16, "w1_bf0_0", 40),
+            (1, 0): staged([P, 4, 16, RUN, PACK], BF16, "w1_bf1_0", 44 - EDGE),
         }
         w1_codes = [sb([P, H], U32, f"w1_codes{a}") for a in range(PASSES)]
         w1_plane = [sb([P, H], U8, f"w1_plane{a}") for a in range(PASSES)]
@@ -237,26 +239,24 @@ def tile_list_pocket_max_affinity_kernel(
                 b_pass(0, s, t)
         for t in range(PACK):
             b_end(0, t, sb([P, HALF], F32, f"b_sb0_{t}"))
-        c_unit(0, 0, sb([P, HALF], F32, "bc_sb0_0"))
-        c_unit(0, 1, sb([P, HALF], F32, "bc_sb0_1"))
-        b_end(1, 0, sb([P, HALF], F32, "b_sb1_0"))
-        c_unit(0, 2, sb([P, HALF], F32, "bc_sb0_2"))
-        b_end(1, 1, sb([P, HALF], F32, "b_sb1_1"))
-        c_unit(0, 3, sb([P, HALF], F32, "bc_sb0_3"))
-        b_end(1, 2, sb([P, HALF], F32, "b_sb1_2"))
-        b_end(1, 3, sb([P, HALF], F32, "b_sb1_3"))
         for t in range(PACK):
-            cast_w1(0, 0, t, True)
+            c_unit(0, t, sb([P, HALF], F32, f"bc_sb0_{t}"))
+        for t in range(PACK):
+            cast_w1(0, 0, t, t > 0)
+        b_end(1, 0, staged([P, HALF], F32, "b_sb1_0", 28))
+        b_end(1, 1, staged([P, HALF], F32, "b_sb1_1", 30))
+        quantize_w1(0, 0, 4)
         for t in range(PACK):
             cast_w1(1, 0, t, t < 2)
-        c_unit(1, 0, sb([P, HALF], F32, "bc_sb1_0"))
-        quantize_w1(0, 0, 4)
-        c_unit(1, 1, staged([P, HALF], F32, "bc_sb1_1", 28))
-        c_unit(1, 2, staged([P, HALF], F32, "bc_sb1_2", 30))
+        b_end(1, 2, staged([P, HALF], F32, "b_sb1_2", 20))
+        b_end(1, 3, staged([P, HALF], F32, "b_sb1_3", 22))
+        c_unit(1, 0, staged([P, HALF], F32, "bc_sb1_0", 38 + EDGE))
+        c_unit(1, 1, staged([P, HALF], F32, "bc_sb1_1", 41))
         quantize_w1(1, 0, 4)
-        c_unit(1, 3, staged([P, HALF], F32, "bc_sb1_3", 32))
+        c_unit(1, 2, staged([P, HALF], F32, "bc_sb1_2", 44))
+        c_unit(1, 3, sb([P, HALF], F32, "bc_sb1_3"))
 
-        wo_bf = staged([P, N, PACK], BF16, "wo_bf", 34)
+        wo_bf = staged([P, N, PACK], BF16, "wo_bf", 46)
         wo_codes = sb([P, N], U32, "wo_codes")
         wo_plane = sb([P, N], U8, "wo_plane")
         nc.gpsimd.tensor_scalar(
@@ -308,17 +308,25 @@ def tile_list_pocket_max_affinity_kernel(
             j0, width = PIECES[n]
             s, c0 = divmod(j0, HALF)
             h_rows = sb([P, PACK, width], BF16, f"h_rows{n}")
+            accs = [bank(A_BANKS[(PACK * n + t) % len(A_BANKS)], f"acc_a{n}_{t}") for t in range(PACK)]
+
+            def a_pass(a, t):
+                product(
+                    accs[t],
+                    w1_codes[a][:, t * P : (t + 1) * P].bitcast(FP8X4),
+                    w1_plane[a][:, t * P : (t + 1) * P],
+                    a, j0, width,
+                )
+
+            if n == 0:
+                for t in range(PACK):
+                    a_pass(0, t)
             for t in range(PACK):
-                acc = bank((PACK * n + t) % 6, f"acc_a{n}_{t}")
-                for a in range(PASSES):
-                    product(
-                        acc,
-                        w1_codes[a][:, t * P : (t + 1) * P].bitcast(FP8X4),
-                        w1_plane[a][:, t * P : (t + 1) * P],
-                        a, j0, width,
-                    )
+                if n > 0:
+                    a_pass(0, t)
+                a_pass(1, t)
                 nc.vector.scalar_tensor_tensor(
-                    h_rows[:, t, :], acc[:, :width], bh_cols[t], bc_sb[s, t][:, c0 : c0 + width], ADD, MAX
+                    h_rows[:, t, :], accs[t][:, :width], bh_cols[t], bc_sb[s, t][:, c0 : c0 + width], ADD, MAX
                 )
             return h_rows
 

@@ -30,7 +30,6 @@ PIECES = [(0, 256), (256, 256), (512, 256), (768, 128), (896, 128)]
 KIB = 1024
 A_BANKS = [4, 5, 0, 1, 2, 3]
 Y_LAST = [(2, 3), (0, 1)]
-EDGE = 1 / 16
 
 
 def tile_list_pocket_max_affinity_kernel(
@@ -46,7 +45,7 @@ def tile_list_pocket_max_affinity_kernel(
             return keep.tile(shape, dtype, name=name, align_bytes=64)
 
         def staged(shape, dtype, name, kib):
-            return stage.tile(shape, dtype, name=name, offset=int(kib * KIB), align_bytes=64)
+            return stage.tile(shape, dtype, name=name, offset=kib * KIB, align_bytes=64)
 
         def bank(n, name):
             return psum.tile([P, HALF], F32, name=name, offset=2 * KIB * n)
@@ -109,7 +108,7 @@ def tile_list_pocket_max_affinity_kernel(
         load_scales(w3_plane_raw, w3_scales, range(4))
 
         w1_rows = w1.rearrange("(a p j) c -> a p j c", p=P, j=PACK)
-        w1_raw = [staged([P, PACK, H], F32, "w1_raw0", 28), staged([P, PACK, H], F32, "w1_raw1", 20)]
+        w1_raw = [staged([P, PACK, H], F32, "w1_raw0", 28), sb([P, PACK, H], F32, "w1_raw1")]
         for a in range(PASSES):
             nc.sync.dma_start(out=w1_raw[a][:], in_=w1_rows[a])
         wo_raw = sb([P, PACK, N], F32, "wo_raw")
@@ -201,7 +200,8 @@ def tile_list_pocket_max_affinity_kernel(
 
         w1_bf = {
             (0, 0): staged([P, 4, 16, RUN, PACK], BF16, "w1_bf0_0", 40),
-            (1, 0): staged([P, 4, 16, RUN, PACK], BF16, "w1_bf1_0", 44 - EDGE),
+            (1, 0): staged([P, 2, 16, RUN, PACK], BF16, "w1_bf1_0", 40),
+            (1, 2): staged([P, 2, 16, RUN, PACK], BF16, "w1_bf1_2", 42),
         }
         w1_codes = [sb([P, H], U32, f"w1_codes{a}") for a in range(PASSES)]
         w1_plane = [sb([P, H], U8, f"w1_plane{a}") for a in range(PASSES)]
@@ -246,17 +246,20 @@ def tile_list_pocket_max_affinity_kernel(
         b_end(1, 0, staged([P, HALF], F32, "b_sb1_0", 28))
         b_end(1, 1, staged([P, HALF], F32, "b_sb1_1", 30))
         quantize_w1(0, 0, 4)
-        for t in range(PACK):
-            cast_w1(1, 0, t, t < 2)
-        b_end(1, 2, staged([P, HALF], F32, "b_sb1_2", 20))
-        b_end(1, 3, staged([P, HALF], F32, "b_sb1_3", 22))
-        c_unit(1, 0, staged([P, HALF], F32, "bc_sb1_0", 38 + EDGE))
-        c_unit(1, 1, staged([P, HALF], F32, "bc_sb1_1", 41))
-        quantize_w1(1, 0, 4)
-        c_unit(1, 2, staged([P, HALF], F32, "bc_sb1_2", 44))
+        cast_w1(1, 0, 0, True)
+        cast_w1(1, 0, 1, True)
+        cast_w1(1, 2, 2, False)
+        b_end(1, 2, staged([P, HALF], F32, "b_sb1_2", 32))
+        cast_w1(1, 2, 3, False)
+        b_end(1, 3, staged([P, HALF], F32, "b_sb1_3", 34))
+        c_unit(1, 0, sb([P, HALF], F32, "bc_sb1_0"))
+        c_unit(1, 1, sb([P, HALF], F32, "bc_sb1_1"))
+        quantize_w1(1, 0, 2)
+        c_unit(1, 2, sb([P, HALF], F32, "bc_sb1_2"))
+        quantize_w1(1, 2, 4)
         c_unit(1, 3, sb([P, HALF], F32, "bc_sb1_3"))
 
-        wo_bf = staged([P, N, PACK], BF16, "wo_bf", 46)
+        wo_bf = staged([P, N, PACK], BF16, "wo_bf", 42)
         wo_codes = sb([P, N], U32, "wo_codes")
         wo_plane = sb([P, N], U8, "wo_plane")
         nc.gpsimd.tensor_scalar(

@@ -337,7 +337,7 @@ def tile_list_pocket_max_affinity_kernel(
         for n in range(len(PIECES) + LAG):
             if n < len(PIECES):
                 rows[n] = third_pocket(n)
-            if n == 0:
+            if n == LAG:
                 nc.vector.quantize_mx(
                     out=wo_codes[:].bitcast(FP8X4), scales=wo_plane[:], in_=wo_bf[:].rearrange("p n t -> p (n t)")
                 )

@@ -242,7 +242,7 @@ def tile_list_pocket_max_affinity_kernel(
         for t in range(PACK):
             c_unit(0, t, sb([P, HALF], F32, f"bc_sb0_{t}"))
         for t in range(PACK):
-            cast_w1(0, 0, t, t > 0)
+            cast_w1(0, 0, t, t >= 2)
         b_end(1, 0, staged([P, HALF], F32, "b_sb1_0", 28))
         b_end(1, 1, staged([P, HALF], F32, "b_sb1_1", 30))
         quantize_w1(0, 0, 4)

@@ -65,13 +65,15 @@ def tile_list_pocket_max_affinity_kernel(
         nc.sync.dma_start(offsets[:], offs)
 
         tab_plane = sb([P, T], U8, "tab_plane")
-        w2_plane_raw = staged([P, PASSES, H], U8, "w2_plane_raw", 16)
-        w3_plane_raw = staged([P, PASSES, H], U8, "w3_plane_raw", 18)
+        w2_plane_raw = staged([P, PASSES, H], U8, "w2_plane_raw", 18)
+        w3_plane_raw = staged([P, PASSES, H], U8, "w3_plane_raw", 16)
         v_plane_low = sb([P, S], U8, "v_plane_low")
+        bh_rows = sb([P, P], F32, "bh_rows")
+        w3_raw = sb([P, PASSES, 2 * H], U8, "w3_raw")
+        nc.sync.dma_start(out=w3_raw[:].bitcast(I32), in_=w3_words.rearrange("a p b -> p a b").bitcast(I32))
         nc.gpsimd.memset(tab_plane[:, 0 : T // 2].bitcast(I32), 0)
         nc.vector.memset(tab_plane[:, T // 2 : T].bitcast(I32), 0)
-        bh_rows = sb([P, P], F32, "bh_rows")
-        nc.vector.memset(bh_rows[:], 0.0)
+        nc.gpsimd.memset(bh_rows[:], 0.0)
         nc.vector.memset(w2_plane_raw[:].bitcast(I32), 0)
         nc.vector.memset(w3_plane_raw[:].bitcast(I32), 0)
         nc.vector.memset(v_plane_low[:].bitcast(I32), 0)
@@ -87,25 +89,35 @@ def tile_list_pocket_max_affinity_kernel(
         tab_rows = tab_words.rearrange("a p t i -> a p (t i)").bitcast(I32)
         tab = [staged([P, T], I32, f"tab{a}", 8 * a) for a in range(PASSES)]
         nc.sync.dma_start(out=tab[0][:], in_=tab_rows[0])
-        w2_raw = sb([P, PASSES, 4 * H], U8, "w2_raw")
-        nc.sync.dma_start(
-            out=w2_raw[:].bitcast(I32), in_=w2_words.rearrange("a p e i -> p a (e i)").bitcast(I32)
-        )
         nc.sync.dma_start(
             out=bh_rows[0:PACK, :].rearrange("t (q i) -> t q i", i=RUN),
             in_=bh.rearrange("(q t i) -> t q i", t=PACK, i=RUN),
         )
-        load_scales(w2_plane_raw, w2_scales, range(4))
+        load_scales(w3_plane_raw, w3_scales, range(4))
         nc.sync.dma_start(out=tab[1][:], in_=tab_rows[1])
-        w3_raw = sb([P, PASSES, 2 * H], U8, "w3_raw")
-        nc.sync.dma_start(out=w3_raw[:].bitcast(I32), in_=w3_words.rearrange("a p b -> p a b").bitcast(I32))
+
+        acc_warm = bank(6, "acc_warm")
+        for n in range(5):
+            nc.tensor.matmul_mx(
+                out=acc_warm[:],
+                lhsT=v_plane_low[:, 0 : PACK * P].bitcast(FP8X4),
+                lhsT_scale=tab_plane[:, 0:P],
+                rhs=w3_raw[:, 0, :].bitcast(FP4X4),
+                rhs_scale=tab_plane[:, 0:HALF],
+                start=True,
+                stop=True,
+            )
 
         picks = [offsets[:, s * HALF // 16 : (s + 1) * HALF // 16] for s in range(HALVES)]
         v_plane = sb([P, S], U8, "v_plane")
         nc.vector.tensor_copy(v_plane[:], tab_plane[:].indirect(offsets[:]))
         nc.sync.dma_start(out=v_plane_low[0:112, :].bitcast(I32), in_=v_plane[16:P, :].bitcast(I32))
         v_planes = [v_plane, v_plane_low]
-        load_scales(w3_plane_raw, w3_scales, range(4))
+        w2_raw = sb([P, PASSES, 4 * H], U8, "w2_raw")
+        nc.sync.dma_start(
+            out=w2_raw[:].bitcast(I32), in_=w2_words.rearrange("a p e i -> p a (e i)").bitcast(I32)
+        )
+        load_scales(w2_plane_raw, w2_scales, range(4))
 
         w1_rows = w1.rearrange("(a p j) c -> a p j c", p=P, j=PACK)
         w1_raw = [staged([P, PACK, H], F32, "w1_raw0", 28), sb([P, PACK, H], F32, "w1_raw1")]
@@ -118,18 +130,6 @@ def tile_list_pocket_max_affinity_kernel(
         bo_col = sb([P, N // P], F32, "bo_col")
         with nc.allow_non_contiguous_dma(reason="one bias value a partition"):
             nc.sync.dma_start(out=bo_col[:], in_=bo.rearrange("(u p) -> p u", p=P))
-
-        acc_warm = bank(6, "acc_warm")
-        for n in range(4):
-            nc.tensor.matmul_mx(
-                out=acc_warm[:],
-                lhsT=tab[0][:, 0:P].bitcast(FP8X4),
-                lhsT_scale=tab_plane[:, 0:P],
-                rhs=tab[0][:, 0:HALF].bitcast(FP8X4),
-                rhs_scale=tab_plane[:, 0:HALF],
-                start=True,
-                stop=True,
-            )
 
         bh_turned = bank(7, "bh_turned")
         nc.tensor.transpose(bh_turned[:, 0:P], bh_rows[:], identity[:])
@@ -144,16 +144,16 @@ def tile_list_pocket_max_affinity_kernel(
             nc.vector.tensor_copy(dst[:], tab[a][:].bitcast(U32).indirect(picks[s]))
 
         gather_words(0, 0, sb([P, HALF], U32, "v_codes0_0"))
-        w2_codes = sb([P, PASSES, 4 * H], U8, "w2_codes")
-        w2_plane = sb([P, PASSES, H], U8, "w2_plane")
-        regroup(w2_codes, w2_raw)
-        regroup(w2_plane, w2_plane_raw)
-        gather_words(0, 1, staged([P, HALF], U32, "v_codes0_1", 16))
-        gather_words(1, 0, sb([P, HALF], U32, "v_codes1_0"))
         w3_codes = sb([P, PASSES, 2 * H], U8, "w3_codes")
         w3_plane = sb([P, PASSES, H], U8, "w3_plane")
         regroup(w3_codes, w3_raw)
         regroup(w3_plane, w3_plane_raw)
+        gather_words(0, 1, staged([P, HALF], U32, "v_codes0_1", 16))
+        gather_words(1, 0, sb([P, HALF], U32, "v_codes1_0"))
+        w2_codes = sb([P, PASSES, 4 * H], U8, "w2_codes")
+        w2_plane = sb([P, PASSES, H], U8, "w2_plane")
+        regroup(w2_codes, w2_raw)
+        regroup(w2_plane, w2_plane_raw)
         gather_words(1, 1, staged([P, HALF], U32, "v_codes1_1", 18))
 
         def product(acc, codes, plane, a, j0, width):
@@ -175,8 +175,8 @@ def tile_list_pocket_max_affinity_kernel(
                 acc_b[s, t] = bank(PACK * s + t, f"acc_b{s}_{t}")
             product(
                 acc_b[s, t],
-                w2_codes[:, a, t * 512 : (t + 1) * 512].bitcast(FP8X4),
-                w2_plane[:, a, t * P : (t + 1) * P],
+                w3_codes[:, a, t * 256 : (t + 1) * 256].bitcast(FP4X4),
+                w3_plane[:, a, t * P : (t + 1) * P],
                 a, s * HALF, HALF,
             )
 
@@ -189,8 +189,8 @@ def tile_list_pocket_max_affinity_kernel(
                 acc_c[s, t] = bank(t, f"acc_c{s}_{t}")
             product(
                 acc_c[s, t],
-                w3_codes[:, a, t * 256 : (t + 1) * 256].bitcast(FP4X4),
-                w3_plane[:, a, t * P : (t + 1) * P],
+                w2_codes[:, a, t * 512 : (t + 1) * 512].bitcast(FP8X4),
+                w2_plane[:, a, t * P : (t + 1) * P],
                 a, s * HALF, HALF,
             )
 

@@ -111,16 +111,16 @@ def tile_list_pocket_max_affinity_kernel(
         picks = [offsets[:, s * HALF // 16 : (s + 1) * HALF // 16] for s in range(HALVES)]
         v_plane = sb([P, S], U8, "v_plane")
         nc.vector.tensor_copy(v_plane[:], tab_plane[:].indirect(offsets[:]))
-        nc.sync.dma_start(out=v_plane_low[0:112, :].bitcast(I32), in_=v_plane[16:P, :].bitcast(I32))
-        v_planes = [v_plane, v_plane_low]
         w2_raw = sb([P, PASSES, 4 * H], U8, "w2_raw")
         nc.sync.dma_start(
             out=w2_raw[:].bitcast(I32), in_=w2_words.rearrange("a p e i -> p a (e i)").bitcast(I32)
         )
+        nc.sync.dma_start(out=v_plane_low[0:112, :].bitcast(I32), in_=v_plane[16:P, :].bitcast(I32))
+        v_planes = [v_plane, v_plane_low]
         load_scales(w2_plane_raw, w2_scales, range(4))
 
         w1_rows = w1.rearrange("(a p j) c -> a p j c", p=P, j=PACK)
-        w1_raw = [staged([P, PACK, H], F32, "w1_raw0", 28), sb([P, PACK, H], F32, "w1_raw1")]
+        w1_raw = [staged([P, PACK, H], F32, "w1_raw0", 28), staged([P, PACK, H], F32, "w1_raw1", 44)]
         for a in range(PASSES):
             nc.sync.dma_start(out=w1_raw[a][:], in_=w1_rows[a])
         wo_raw = sb([P, PACK, N], F32, "wo_raw")
@@ -199,9 +199,10 @@ def tile_list_pocket_max_affinity_kernel(
             nc.vector.scalar_tensor_tensor(dst[:], acc_c[s, t][:], bh_cols[t], b_sb[s, t][:], ADD, MAX)
 
         w1_bf = {
-            (0, 0): staged([P, 4, 16, RUN, PACK], BF16, "w1_bf0_0", 40),
+            (0, 0): staged([P, 2, 16, RUN, PACK], BF16, "w1_bf0_0", 42),
+            (0, 2): staged([P, 2, 16, RUN, PACK], BF16, "w1_bf0_2", 40),
             (1, 0): staged([P, 2, 16, RUN, PACK], BF16, "w1_bf1_0", 40),
-            (1, 2): staged([P, 2, 16, RUN, PACK], BF16, "w1_bf1_2", 42),
+            (1, 2): staged([P, 2, 16, RUN, PACK], BF16, "w1_bf1_2", 40),
         }
         w1_codes = [sb([P, H], U32, f"w1_codes{a}") for a in range(PASSES)]
         w1_plane = [sb([P, H], U8, f"w1_plane{a}") for a in range(PASSES)]
@@ -240,30 +241,30 @@ def tile_list_pocket_max_affinity_kernel(
         for t in range(PACK):
             b_end(0, t, sb([P, HALF], F32, f"b_sb0_{t}"))
         for t in range(PACK):
-            c_unit(0, t, sb([P, HALF], F32, f"bc_sb0_{t}"))
+            cast_w1(0, t - t % 2, t, t >= 2)
         for t in range(PACK):
-            cast_w1(0, 0, t, t >= 2)
-        b_end(1, 0, staged([P, HALF], F32, "b_sb1_0", 28))
-        b_end(1, 1, staged([P, HALF], F32, "b_sb1_1", 30))
-        quantize_w1(0, 0, 4)
+            c_unit(0, t, sb([P, HALF], F32, f"bc_sb0_{t}"))
+            if t >= 2:
+                quantize_w1(0, 6 - 2 * t, 8 - 2 * t)
+        for t in range(PACK):
+            b_end(1, t, staged([P, HALF], F32, f"b_sb1_{t}", 28 + 2 * t))
         cast_w1(1, 0, 0, True)
         cast_w1(1, 0, 1, True)
-        cast_w1(1, 2, 2, False)
-        b_end(1, 2, staged([P, HALF], F32, "b_sb1_2", 32))
-        cast_w1(1, 2, 3, False)
-        b_end(1, 3, staged([P, HALF], F32, "b_sb1_3", 34))
         c_unit(1, 0, sb([P, HALF], F32, "bc_sb1_0"))
         c_unit(1, 1, sb([P, HALF], F32, "bc_sb1_1"))
         quantize_w1(1, 0, 2)
+        cast_w1(1, 2, 2, True)
+        cast_w1(1, 2, 3, False)
         c_unit(1, 2, sb([P, HALF], F32, "bc_sb1_2"))
-        quantize_w1(1, 2, 4)
         c_unit(1, 3, sb([P, HALF], F32, "bc_sb1_3"))
+        quantize_w1(1, 2, 4)
 
-        wo_bf = staged([P, N, PACK], BF16, "wo_bf", 42)
+        wo_bf = staged([P, N, PACK], BF16, "wo_bf", 44)
         wo_codes = sb([P, N], U32, "wo_codes")
         wo_plane = sb([P, N], U8, "wo_plane")
-        nc.gpsimd.tensor_scalar(
-            out=wo_bf[:], in0=wo_raw[:].rearrange("p t n -> p n t"), scalar1=1.0, scalar2=0.0, op0=MULT, op1=ADD
+        nc.scalar.copy(
+            out=wo_bf[:].rearrange("p (c i) t -> p c t i", i=4),
+            in_=wo_raw[:].rearrange("p t (c i) -> p c t i", i=4),
         )
 
         out_rows = out.rearrange("(u p) s -> p u s", p=P)
@@ -273,7 +274,7 @@ def tile_list_pocket_max_affinity_kernel(
             h_bf = sb([P, width, PACK], BF16, f"h_bf{n}")
             last = n >= len(PIECES) - 2
             final = n == len(PIECES) - 1
-            (nc.vector.tensor_copy if final else nc.scalar.copy)(
+            (nc.vector.tensor_copy if last else nc.scalar.copy)(
                 out=h_bf[:].rearrange("p (c i) t -> p c t i", i=4),
                 in_=h_rows[:].rearrange("p t (c i) -> p c t i", i=4),
             )

@@ -25,11 +25,11 @@ PASSES = K // (P * PACK)
 RUN = 8
 HALF = 512
 HALVES = S // HALF
-LAG = 1
 PIECES = [(0, 256), (256, 256), (512, 256), (768, 128), (896, 128)]
 KIB = 1024
+LAG = 2
 A_BANKS = [4, 5, 0, 1, 2, 3]
-Y_LAST = [(2, 3), (0, 1)]
+Y_LAST = [(2, 3), (0, 1), (4, 5)]
 
 
 def tile_list_pocket_max_affinity_kernel(
@@ -196,20 +196,20 @@ def tile_list_pocket_max_affinity_kernel(
 
         def c_out(s, t, dst):
             bc_sb[s, t] = dst
-            nc.vector.scalar_tensor_tensor(dst[:], acc_c[s, t][:], bh_cols[t], b_sb[s, t][:], ADD, MAX)
+            nc.vector.scalar_tensor_tensor(dst, acc_c[s, t][:], bh_cols[t], b_sb[s, t][:], ADD, MAX)
 
+        shared = sb([P, (PACK + 1) * HALF], F32, "shared")
         w1_bf = {
-            (0, 0): staged([P, 2, 16, RUN, PACK], BF16, "w1_bf0_0", 42),
-            (0, 2): staged([P, 2, 16, RUN, PACK], BF16, "w1_bf0_2", 40),
-            (1, 0): staged([P, 2, 16, RUN, PACK], BF16, "w1_bf1_0", 40),
-            (1, 2): staged([P, 2, 16, RUN, PACK], BF16, "w1_bf1_2", 40),
+            (0, 0): sb([P, 2 * H], BF16, "w1_bf0_0")[:],
+            (0, 2): shared[:, 3 * HALF : 4 * HALF].bitcast(BF16),
+            (1, 0): shared[:, 3 * HALF : 5 * HALF].bitcast(BF16),
         }
         w1_codes = [sb([P, H], U32, f"w1_codes{a}") for a in range(PASSES)]
         w1_plane = [sb([P, H], U8, f"w1_plane{a}") for a in range(PASSES)]
 
         def cast_w1(a, t0, t, on_gpsimd):
             src = w1_raw[a][:].rearrange("p j (q t i) -> p t q i j", t=PACK, i=RUN)[:, t]
-            dst = w1_bf[a, t0][:, t - t0]
+            dst = w1_bf[a, t0][:, (t - t0) * H : (t - t0 + 1) * H].rearrange("p (q i j) -> p q i j", i=RUN, j=PACK)
             if on_gpsimd:
                 nc.gpsimd.tensor_scalar(out=dst, in0=src, scalar1=1.0, scalar2=0.0, op0=MULT, op1=ADD)
             else:
@@ -220,7 +220,7 @@ def tile_list_pocket_max_affinity_kernel(
             nc.vector.quantize_mx(
                 out=w1_codes[a][:, t0 * P : t1 * P].bitcast(FP8X4),
                 scales=w1_plane[a][:, t0 * P : t1 * P],
-                in_=w1_bf[a, t0][:].rearrange("p t q i j -> p (t q i j)"),
+                in_=w1_bf[a, t0],
             )
 
         def whole(one_pass, s, t):
@@ -243,21 +243,17 @@ def tile_list_pocket_max_affinity_kernel(
         for t in range(PACK):
             cast_w1(0, t - t % 2, t, t >= 2)
         for t in range(PACK):
-            c_unit(0, t, sb([P, HALF], F32, f"bc_sb0_{t}"))
+            c_unit(0, t, sb([P, HALF], F32, f"bc_sb0_{t}")[:])
             if t >= 2:
                 quantize_w1(0, 6 - 2 * t, 8 - 2 * t)
         for t in range(PACK):
             b_end(1, t, staged([P, HALF], F32, f"b_sb1_{t}", 28 + 2 * t))
-        cast_w1(1, 0, 0, True)
-        cast_w1(1, 0, 1, True)
-        c_unit(1, 0, sb([P, HALF], F32, "bc_sb1_0"))
-        c_unit(1, 1, sb([P, HALF], F32, "bc_sb1_1"))
-        quantize_w1(1, 0, 2)
-        cast_w1(1, 2, 2, True)
-        cast_w1(1, 2, 3, False)
-        c_unit(1, 2, sb([P, HALF], F32, "bc_sb1_2"))
-        c_unit(1, 3, sb([P, HALF], F32, "bc_sb1_3"))
-        quantize_w1(1, 2, 4)
+        for t in range(PACK):
+            cast_w1(1, 0, t, t < 3)
+        for t in range(PACK):
+            if t == 3:
+                quantize_w1(1, 0, 4)
+            c_unit(1, t, shared[:, t * HALF : (t + 1) * HALF])
 
         wo_bf = staged([P, N, PACK], BF16, "wo_bf", 44)
         wo_codes = sb([P, N], U32, "wo_codes")
@@ -274,10 +270,13 @@ def tile_list_pocket_max_affinity_kernel(
             h_bf = sb([P, width, PACK], BF16, f"h_bf{n}")
             last = n >= len(PIECES) - 2
             final = n == len(PIECES) - 1
-            (nc.vector.tensor_copy if last else nc.scalar.copy)(
-                out=h_bf[:].rearrange("p (c i) t -> p c t i", i=4),
-                in_=h_rows[:].rearrange("p t (c i) -> p c t i", i=4),
-            )
+            woven = h_bf[:].rearrange("p (c i) t -> p c t i", i=4)
+            rows_in = h_rows[:].rearrange("p t (c i) -> p c t i", i=4)
+            if final:
+                other = bc_high[:, :, j0 - HALF : j0 - HALF + width].rearrange("p t (c i) -> p c t i", i=4)
+                nc.vector.tensor_tensor(woven, rows_in, other, MAX)
+            else:
+                (nc.vector.tensor_copy if last else nc.scalar.copy)(out=woven, in_=rows_in)
             h_codes = sb([P, width], U32, f"h_codes{n}")
             h_plane = sb([P, width], U8, f"h_plane{n}")
             nc.vector.quantize_mx(
@@ -286,8 +285,8 @@ def tile_list_pocket_max_affinity_kernel(
             y = sb([P, N // P, width], F32, f"y{n}")
             accs = []
             for u in range(N // P):
-                if last:
-                    accs.append(bank(Y_LAST[n % 2][u], f"acc_y{n}_{u}")[:, 0:width])
+                if n >= 2:
+                    accs.append(bank(Y_LAST[n - 2][u], f"acc_y{n}_{u}")[:, 0:width])
                 else:
                     if u == 0:
                         both = bank(6 + n % 2, f"acc_y{n}")
@@ -302,7 +301,7 @@ def tile_list_pocket_max_affinity_kernel(
                     stop=True,
                 )
             for u in range(N // P):
-                if final and u == 1:
+                if n >= 2 and u == 1:
                     nc.vector.tensor_scalar_add(y[:, u, :], accs[u], bo_col[:, u : u + 1])
                 else:
                     nc.scalar.activation(y[:, u, :], accs[u], IDENT, bias=bo_col[:, u : u + 1])
@@ -334,10 +333,29 @@ def tile_list_pocket_max_affinity_kernel(
                 )
             return h_rows
 
+        def early_piece(n):
+            j0, width = PIECES[n]
+            a_rows = sb([P, PACK, width], F32, "a_rows")
+            acc = bank(7, "acc_early")
+            for t in range(PACK):
+                for a in range(PASSES):
+                    product(
+                        acc[:, t * width : (t + 1) * width],
+                        w1_codes[a][:, t * P : (t + 1) * P].bitcast(FP8X4),
+                        w1_plane[a][:, t * P : (t + 1) * P],
+                        a, j0, width,
+                    )
+            for t in range(PACK):
+                nc.scalar.activation(a_rows[:, t, :], acc[:, t * width : (t + 1) * width], IDENT, bias=bh_cols[t])
+            return a_rows
+
+        bc_high = shared[:, 0 : PACK * HALF].rearrange("p (t n) -> p t n", t=PACK)
         rows = {}
         for n in range(len(PIECES) + LAG):
-            if n < len(PIECES):
+            if n < len(PIECES) - 1:
                 rows[n] = third_pocket(n)
+            if n == 0:
+                rows[len(PIECES) - 1] = early_piece(len(PIECES) - 1)
             if n == LAG:
                 nc.vector.quantize_mx(
                     out=wo_codes[:].bitcast(FP8X4), scales=wo_plane[:], in_=wo_bf[:].rearrange("p n t -> p (n t)")

@@ -28,7 +28,7 @@ HALVES = S // HALF
 PIECES = [(0, 256), (256, 256), (512, 256), (768, 128), (896, 128)]
 KIB = 1024
 LAG = 2
-A_BANKS = [4, 5, 0, 1, 2, 3]
+A_BANKS = [4, 3, 5, 0, 1, 2]
 Y_LAST = [(2, 3), (0, 1), (4, 5)]
 
 
@@ -184,9 +184,9 @@ def tile_list_pocket_max_affinity_kernel(
             b_sb[s, t] = dst
             nc.scalar.activation(dst[:], acc_b[s, t][:], IDENT, bias=bh_cols[t])
 
-        def c_pass(a, s, t):
+        def c_pass(a, s, t, where):
             if a == 0:
-                acc_c[s, t] = bank(t, f"acc_c{s}_{t}")
+                acc_c[s, t] = bank(where, f"acc_c{s}_{t}")
             product(
                 acc_c[s, t],
                 w2_codes[:, a, t * 512 : (t + 1) * 512].bitcast(FP8X4),
@@ -198,62 +198,73 @@ def tile_list_pocket_max_affinity_kernel(
             bc_sb[s, t] = dst
             nc.vector.scalar_tensor_tensor(dst, acc_c[s, t][:], bh_cols[t], b_sb[s, t][:], ADD, MAX)
 
-        shared = sb([P, (PACK + 1) * HALF], F32, "shared")
-        w1_bf = {
-            (0, 0): sb([P, 2 * H], BF16, "w1_bf0_0")[:],
-            (0, 2): shared[:, 3 * HALF : 4 * HALF].bitcast(BF16),
-            (1, 0): shared[:, 3 * HALF : 5 * HALF].bitcast(BF16),
-        }
-        w1_codes = [sb([P, H], U32, f"w1_codes{a}") for a in range(PASSES)]
-        w1_plane = [sb([P, H], U8, f"w1_plane{a}") for a in range(PASSES)]
+        shared = sb([P, PACK * HALF], F32, "shared")
+        w1_bf = sb([P, PACK * PASSES * H], BF16, "w1_bf")
+        w1_codes = sb([P, PACK * PASSES * P], U32, "w1_codes")
+        w1_plane = sb([P, PACK * PASSES * P], U8, "w1_plane")
 
-        def cast_w1(a, t0, t, on_gpsimd):
-            src = w1_raw[a][:].rearrange("p j (q t i) -> p t q i j", t=PACK, i=RUN)[:, t]
-            dst = w1_bf[a, t0][:, (t - t0) * H : (t - t0 + 1) * H].rearrange("p (q i j) -> p q i j", i=RUN, j=PACK)
-            if on_gpsimd:
-                nc.gpsimd.tensor_scalar(out=dst, in0=src, scalar1=1.0, scalar2=0.0, op0=MULT, op1=ADD)
-            else:
-                order = "p q (h i) j -> p q h j i"
-                nc.scalar.copy(out=dst.rearrange(order, h=2), in_=src.rearrange(order, h=2))
+        def cast_views(a):
+            src = w1_raw[a][:].rearrange("p j (q t i) -> p q t i j", t=PACK, i=RUN)
+            dst = w1_bf[:].rearrange("p (t a q i j) -> p a q t i j", t=PACK, a=PASSES, i=RUN, j=PACK)[:, a]
+            return src, dst
 
-        def quantize_w1(a, t0, t1):
-            nc.vector.quantize_mx(
-                out=w1_codes[a][:, t0 * P : t1 * P].bitcast(FP8X4),
-                scales=w1_plane[a][:, t0 * P : t1 * P],
-                in_=w1_bf[a, t0],
+        def cast_on_gpsimd(a, t0):
+            src, dst = cast_views(a)
+            nc.gpsimd.tensor_scalar(
+                out=dst[:, :, t0:PACK], in0=src[:, :, t0:PACK], scalar1=1.0, scalar2=0.0, op0=MULT, op1=ADD
             )
 
-        def whole(one_pass, s, t):
-            for a in range(PASSES):
-                one_pass(a, s, t)
+        def cast_on_scalar(a, t):
+            src, dst = cast_views(a)
+            order = "p q (h i) j -> p q h j i"
+            nc.scalar.copy(out=dst[:, :, t].rearrange(order, h=2), in_=src[:, :, t].rearrange(order, h=2))
 
-        def c_unit(s, t, dst):
-            whole(c_pass, s, t)
-            c_out(s, t, dst)
+        def quantize_w1(pair):
+            c0, c1 = 2 * PASSES * P * pair, 2 * PASSES * P * (pair + 1)
+            nc.vector.quantize_mx(
+                out=w1_codes[:, c0:c1].bitcast(FP8X4), scales=w1_plane[:, c0:c1], in_=w1_bf[:, PACK * c0 : PACK * c1]
+            )
+
+        def a_pass(acc, a, t, j0, width):
+            c0 = (PASSES * t + a) * P
+            product(acc, w1_codes[:, c0 : c0 + P].bitcast(FP8X4), w1_plane[:, c0 : c0 + P], a, j0, width)
+
+        def c_passes(s, t, where):
+            for a in range(PASSES):
+                c_pass(a, s, t, where)
 
         def b_end(s, t, dst):
             b_pass(1, s, t)
             b_out(s, t, dst)
 
+        def high(t):
+            return shared[:, t * HALF : (t + 1) * HALF]
+
         for s in range(HALVES):
-            for t in range(PACK):
+            for t in range(PACK - s):
                 b_pass(0, s, t)
         for t in range(PACK):
             b_end(0, t, sb([P, HALF], F32, f"b_sb0_{t}"))
         for t in range(PACK):
-            cast_w1(0, t - t % 2, t, t >= 2)
-        for t in range(PACK):
-            c_unit(0, t, sb([P, HALF], F32, f"bc_sb0_{t}")[:])
-            if t >= 2:
-                quantize_w1(0, 6 - 2 * t, 8 - 2 * t)
-        for t in range(PACK):
-            b_end(1, t, staged([P, HALF], F32, f"b_sb1_{t}", 28 + 2 * t))
-        for t in range(PACK):
-            cast_w1(1, 0, t, t < 3)
-        for t in range(PACK):
+            c_passes(0, t, (t - 1) % 8)
+            c_out(0, t, sb([P, HALF], F32, f"bc_sb0_{t}")[:])
+            if t == 1:
+                b_end(1, 0, sb([P, HALF], F32, "b_sb1_0"))
+        for a in range(PASSES):
+            for t in range(a + 1):
+                cast_on_scalar(a, t)
+            cast_on_gpsimd(a, a + 1)
+        c_passes(1, 0, 3)
+        c_out(1, 0, high(0))
+        quantize_w1(0)
+        quantize_w1(1)
+        for t in range(1, PACK):
             if t == 3:
-                quantize_w1(1, 0, 4)
-            c_unit(1, t, shared[:, t * HALF : (t + 1) * HALF])
+                b_pass(0, 1, t)
+            b_end(1, t, staged([P, HALF], F32, f"b_sb1_{t}", 44 + 2 * t))
+        for t in range(1, PACK):
+            c_passes(1, t, t - 1)
+            c_out(1, t, high(t))
 
         wo_bf = staged([P, N, PACK], BF16, "wo_bf", 44)
         wo_codes = sb([P, N], U32, "wo_codes")
@@ -313,21 +324,9 @@ def tile_list_pocket_max_affinity_kernel(
             h_rows = sb([P, PACK, width], BF16, f"h_rows{n}")
             accs = [bank(A_BANKS[(PACK * n + t) % len(A_BANKS)], f"acc_a{n}_{t}") for t in range(PACK)]
 
-            def a_pass(a, t):
-                product(
-                    accs[t],
-                    w1_codes[a][:, t * P : (t + 1) * P].bitcast(FP8X4),
-                    w1_plane[a][:, t * P : (t + 1) * P],
-                    a, j0, width,
-                )
-
-            if n == 0:
-                for t in range(PACK):
-                    a_pass(0, t)
             for t in range(PACK):
-                if n > 0:
-                    a_pass(0, t)
-                a_pass(1, t)
+                for a in range(PASSES):
+                    a_pass(accs[t], a, t, j0, width)
                 nc.vector.scalar_tensor_tensor(
                     h_rows[:, t, :], accs[t][:, :width], bh_cols[t], bc_sb[s, t][:, c0 : c0 + width], ADD, MAX
                 )
@@ -339,12 +338,7 @@ def tile_list_pocket_max_affinity_kernel(
             acc = bank(7, "acc_early")
             for t in range(PACK):
                 for a in range(PASSES):
-                    product(
-                        acc[:, t * width : (t + 1) * width],
-                        w1_codes[a][:, t * P : (t + 1) * P].bitcast(FP8X4),
-                        w1_plane[a][:, t * P : (t + 1) * P],
-                        a, j0, width,
-                    )
+                    a_pass(acc[:, t * width : (t + 1) * width], a, t, j0, width)
             for t in range(PACK):
                 nc.scalar.activation(a_rows[:, t, :], acc[:, t * width : (t + 1) * width], IDENT, bias=bh_cols[t])
             return a_rows

@@ -27,8 +27,9 @@ HALF = 512
 HALVES = S // HALF
 PIECES = [(0, 256), (256, 256), (512, 256), (768, 128), (896, 128)]
 KIB = 1024
+W2_ROW = 4
 LAG = 2
-A_BANKS = [4, 3, 5, 0, 1, 2]
+A_BANKS = [4, 5, 3, 0, 1, 2]
 Y_LAST = [(2, 3), (0, 1), (4, 5)]
 
 
@@ -50,10 +51,10 @@ def tile_list_pocket_max_affinity_kernel(
         def bank(n, name):
             return psum.tile([P, HALF], F32, name=name, offset=2 * KIB * n)
 
-        def load_scales(plane, scales, which, queue=nc.sync):
+        def load_scales(plane, scales, first, which):
             rows = scales.bitcast(I32).rearrange("a (g r) w -> r g a w", r=4)
             for r in which:
-                queue.dma_start(out=plane[r:P:32, :, :].bitcast(I32), in_=rows[r])
+                nc.sync.dma_start(out=plane[first + r : P : 32, :, :].bitcast(I32), in_=rows[r])
 
         def regroup(dst, src):
             nc.vector.tensor_copy(
@@ -93,7 +94,7 @@ def tile_list_pocket_max_affinity_kernel(
             out=bh_rows[0:PACK, :].rearrange("t (q i) -> t q i", i=RUN),
             in_=bh.rearrange("(q t i) -> t q i", t=PACK, i=RUN),
         )
-        load_scales(w3_plane_raw, w3_scales, range(4))
+        load_scales(w3_plane_raw, w3_scales, 0, range(4))
         nc.sync.dma_start(out=tab[1][:], in_=tab_rows[1])
 
         acc_warm = bank(6, "acc_warm")
@@ -115,9 +116,10 @@ def tile_list_pocket_max_affinity_kernel(
         nc.sync.dma_start(
             out=w2_raw[:].bitcast(I32), in_=w2_words.rearrange("a p e i -> p a (e i)").bitcast(I32)
         )
+        load_scales(w2_plane_raw, w2_scales, W2_ROW, range(3))
         nc.sync.dma_start(out=v_plane_low[0:112, :].bitcast(I32), in_=v_plane[16:P, :].bitcast(I32))
+        load_scales(w2_plane_raw, w2_scales, W2_ROW, range(3, 4))
         v_planes = [v_plane, v_plane_low]
-        load_scales(w2_plane_raw, w2_scales, range(4))
 
         w1_rows = w1.rearrange("(a p j) c -> a p j c", p=P, j=PACK)
         w1_raw = [staged([P, PACK, H], F32, "w1_raw0", 28), staged([P, PACK, H], F32, "w1_raw1", 44)]
@@ -190,7 +192,7 @@ def tile_list_pocket_max_affinity_kernel(
             product(
                 acc_c[s, t],
                 w2_codes[:, a, t * 512 : (t + 1) * 512].bitcast(FP8X4),
-                w2_plane[:, a, t * P : (t + 1) * P],
+                w2_plane[W2_ROW:P, a, t * P : (t + 1) * P],
                 a, s * HALF, HALF,
             )
 
@@ -248,21 +250,22 @@ def tile_list_pocket_max_affinity_kernel(
         for t in range(PACK):
             c_passes(0, t, (t - 1) % 8)
             c_out(0, t, sb([P, HALF], F32, f"bc_sb0_{t}")[:])
-            if t == 1:
-                b_end(1, 0, sb([P, HALF], F32, "b_sb1_0"))
+            if t in (1, 2):
+                b_end(1, t - 1, sb([P, HALF], F32, f"b_sb1_{t - 1}"))
         for a in range(PASSES):
             for t in range(a + 1):
                 cast_on_scalar(a, t)
             cast_on_gpsimd(a, a + 1)
-        c_passes(1, 0, 3)
-        c_out(1, 0, high(0))
+        for t in range(2):
+            c_passes(1, t, 3 - 3 * t)
+            c_out(1, t, high(t))
         quantize_w1(0)
         quantize_w1(1)
-        for t in range(1, PACK):
+        for t in range(2, PACK):
             if t == 3:
                 b_pass(0, 1, t)
             b_end(1, t, staged([P, HALF], F32, f"b_sb1_{t}", 44 + 2 * t))
-        for t in range(1, PACK):
+        for t in range(2, PACK):
             c_passes(1, t, t - 1)
             c_out(1, t, high(t))
 

@@ -56,10 +56,10 @@ def tile_list_pocket_max_affinity_kernel(
             for r in which:
                 nc.sync.dma_start(out=plane[first + r : P : 32, :, :].bitcast(I32), in_=rows[r])
 
-        def regroup(dst, src):
-            nc.vector.tensor_copy(
-                out=dst[:].bitcast(I32).rearrange("p a (t q w) -> p a t q w", t=PACK, q=16),
-                in_=src[:].bitcast(I32).rearrange("p a (q t w) -> p a t q w", t=PACK, q=16),
+        def regroup(dst, src, copy=nc.vector.tensor_copy, dtype=I32):
+            copy(
+                out=dst[:].bitcast(dtype).rearrange("p a (t q w) -> p a t q w", t=PACK, q=16),
+                in_=src[:].bitcast(dtype).rearrange("p a (q t w) -> p a t q w", t=PACK, q=16),
             )
 
         offsets = keep.tile([P, S // 16], U16, name="offsets")
@@ -146,11 +146,11 @@ def tile_list_pocket_max_affinity_kernel(
             nc.vector.tensor_copy(dst[:], tab[a][:].bitcast(U32).indirect(picks[s]))
 
         gather_words(0, 0, sb([P, HALF], U32, "v_codes0_0"))
+        gather_words(0, 1, sb([P, HALF], U32, "v_codes0_1"))
         w3_codes = sb([P, PASSES, 2 * H], U8, "w3_codes")
         w3_plane = sb([P, PASSES, H], U8, "w3_plane")
-        regroup(w3_codes, w3_raw)
-        regroup(w3_plane, w3_plane_raw)
-        gather_words(0, 1, staged([P, HALF], U32, "v_codes0_1", 16))
+        regroup(w3_codes, w3_raw, nc.scalar.copy, U32)
+        regroup(w3_plane, w3_plane_raw, nc.scalar.copy, U32)
         gather_words(1, 0, sb([P, HALF], U32, "v_codes1_0"))
         w2_codes = sb([P, PASSES, 4 * H], U8, "w2_codes")
         w2_plane = sb([P, PASSES, H], U8, "w2_plane")

@@ -201,7 +201,7 @@ def tile_list_pocket_max_affinity_kernel(
             nc.vector.scalar_tensor_tensor(dst, acc_c[s, t][:], bh_cols[t], b_sb[s, t][:], ADD, MAX)
 
         shared = sb([P, PACK * HALF], F32, "shared")
-        w1_bf = sb([P, PACK * PASSES * H], BF16, "w1_bf")
+        w1_bf = staged([P, PACK * PASSES * H], BF16, "w1_bf", 60)
         w1_codes = sb([P, PACK * PASSES * P], U32, "w1_codes")
         w1_plane = sb([P, PACK * PASSES * P], U8, "w1_plane")
 
@@ -253,9 +253,9 @@ def tile_list_pocket_max_affinity_kernel(
             if t in (1, 2):
                 b_end(1, t - 1, sb([P, HALF], F32, f"b_sb1_{t - 1}"))
         for a in range(PASSES):
-            for t in range(a + 1):
+            for t in range(2 * a + 1):
                 cast_on_scalar(a, t)
-            cast_on_gpsimd(a, a + 1)
+            cast_on_gpsimd(a, 2 * a + 1)
         for t in range(2):
             c_passes(1, t, 3 - 3 * t)
             c_out(1, t, high(t))
@@ -269,12 +269,11 @@ def tile_list_pocket_max_affinity_kernel(
             c_passes(1, t, t - 1)
             c_out(1, t, high(t))
 
-        wo_bf = staged([P, N, PACK], BF16, "wo_bf", 44)
+        wo_bf = staged([P, N, PACK], BF16, "wo_bf", 60)
         wo_codes = sb([P, N], U32, "wo_codes")
         wo_plane = sb([P, N], U8, "wo_plane")
-        nc.scalar.copy(
-            out=wo_bf[:].rearrange("p (c i) t -> p c t i", i=4),
-            in_=wo_raw[:].rearrange("p t (c i) -> p c t i", i=4),
+        nc.gpsimd.tensor_scalar(
+            out=wo_bf[:], in0=wo_raw[:].rearrange("p t n -> p n t"), scalar1=1.0, scalar2=0.0, op0=MULT, op1=ADD
         )
 
         out_rows = out.rearrange("(u p) s -> p u s", p=P)

@@ -78,6 +78,10 @@ def tile_list_pocket_max_affinity_kernel(
         nc.vector.memset(w2_plane_raw[:].bitcast(I32), 0)
         nc.vector.memset(w3_plane_raw[:].bitcast(I32), 0)
         nc.vector.memset(v_plane_low[:].bitcast(I32), 0)
+        w2_codes = sb([P, PASSES, 4 * H], U8, "w2_codes")
+        w2_plane = sb([P, PASSES, H], U8, "w2_plane")
+        nc.vector.memset(w2_codes[:, 0, 0 : PACK * P].bitcast(I32), 0)
+        nc.vector.memset(w2_plane[:, 0, :].bitcast(I32), 0)
         identity = sb([P, P], F32, "identity")
         make_identity(nc, identity[:])
         warm = sb([P, 16], F32, "warm")
@@ -97,18 +101,6 @@ def tile_list_pocket_max_affinity_kernel(
         load_scales(w3_plane_raw, w3_scales, 0, range(4))
         nc.sync.dma_start(out=tab[1][:], in_=tab_rows[1])
 
-        acc_warm = bank(6, "acc_warm")
-        for n in range(5):
-            nc.tensor.matmul_mx(
-                out=acc_warm[:],
-                lhsT=v_plane_low[:, 0 : PACK * P].bitcast(FP8X4),
-                lhsT_scale=tab_plane[:, 0:P],
-                rhs=w3_raw[:, 0, :].bitcast(FP4X4),
-                rhs_scale=tab_plane[:, 0:HALF],
-                start=True,
-                stop=True,
-            )
-
         picks = [offsets[:, s * HALF // 16 : (s + 1) * HALF // 16] for s in range(HALVES)]
         v_plane = sb([P, S], U8, "v_plane")
         nc.vector.tensor_copy(v_plane[:], tab_plane[:].indirect(offsets[:]))
@@ -123,8 +115,10 @@ def tile_list_pocket_max_affinity_kernel(
 
         w1_rows = w1.rearrange("(a p j) c -> a p j c", p=P, j=PACK)
         w1_raw = [staged([P, PACK, H], F32, "w1_raw0", 28), staged([P, PACK, H], F32, "w1_raw1", 44)]
-        for a in range(PASSES):
-            nc.sync.dma_start(out=w1_raw[a][:], in_=w1_rows[a])
+        nc.sync.dma_start(out=w1_raw[0][:], in_=w1_rows[0])
+        for h in range(2):
+            cols = slice(h * H // 2, (h + 1) * H // 2)
+            nc.sync.dma_start(out=w1_raw[1][:, :, cols], in_=w1_rows[1][:, :, cols])
         wo_raw = sb([P, PACK, N], F32, "wo_raw")
         wo_rows = wo.rearrange("(q t i) n -> t q i n", t=PACK, i=RUN)
         for t in range(PACK):
@@ -150,10 +144,20 @@ def tile_list_pocket_max_affinity_kernel(
         w3_codes = sb([P, PASSES, 2 * H], U8, "w3_codes")
         w3_plane = sb([P, PASSES, H], U8, "w3_plane")
         regroup(w3_codes, w3_raw, nc.scalar.copy, U32)
+        acc_warm = bank(6, "acc_warm")
+        for n in range(5):
+            nc.tensor.matmul_mx(
+                out=acc_warm[:],
+                lhsT=w2_codes[:, 0, 0 : PACK * P].bitcast(FP8X4),
+                lhsT_scale=w2_plane[:, 0, 0:P],
+                rhs=w3_codes[:, 0, :].bitcast(FP4X4),
+                rhs_scale=w2_plane[:, 0, :],
+                start=True,
+                stop=True,
+            )
+
         regroup(w3_plane, w3_plane_raw, nc.scalar.copy, U32)
         gather_words(1, 0, sb([P, HALF], U32, "v_codes1_0"))
-        w2_codes = sb([P, PASSES, 4 * H], U8, "w2_codes")
-        w2_plane = sb([P, PASSES, H], U8, "w2_plane")
         regroup(w2_codes, w2_raw)
         regroup(w2_plane, w2_plane_raw)
         gather_words(1, 1, staged([P, HALF], U32, "v_codes1_1", 18))
@@ -221,6 +225,12 @@ def tile_list_pocket_max_affinity_kernel(
             order = "p q (h i) j -> p q h j i"
             nc.scalar.copy(out=dst[:, :, t].rearrange(order, h=2), in_=src[:, :, t].rearrange(order, h=2))
 
+        def cast_half_on_scalar(h, t0, t1):
+            src, dst = cast_views(1)
+            order = "p q t i j -> p q t j i"
+            blocks = slice(8 * h, 8 * h + 8)
+            nc.scalar.copy(out=dst[:, blocks, t0:t1].rearrange(order), in_=src[:, blocks, t0:t1].rearrange(order))
+
         def quantize_w1(pair):
             c0, c1 = 2 * PASSES * P * pair, 2 * PASSES * P * (pair + 1)
             nc.vector.quantize_mx(
@@ -252,10 +262,12 @@ def tile_list_pocket_max_affinity_kernel(
             c_out(0, t, sb([P, HALF], F32, f"bc_sb0_{t}")[:])
             if t in (1, 2):
                 b_end(1, t - 1, sb([P, HALF], F32, f"b_sb1_{t - 1}"))
-        for a in range(PASSES):
-            for t in range(2 * a + 1):
-                cast_on_scalar(a, t)
-            cast_on_gpsimd(a, 2 * a + 1)
+        cast_on_scalar(0, 0)
+        cast_on_gpsimd(0, 1)
+        cast_half_on_scalar(0, 0, 3)
+        cast_half_on_scalar(1, 0, 2)
+        cast_half_on_scalar(1, 2, 3)
+        cast_on_gpsimd(1, 3)
         for t in range(2):
             c_passes(1, t, 3 - 3 * t)
             c_out(1, t, high(t))

from contextlib import ExitStack

import concourse.mybir as mybir
from concourse.masks import make_identity

K, T, S, H, N = 1024, 2048, 1024, 512, 256
FLOPS = 2 * 3 * K * H * S + 2 * H * N * S

F32 = mybir.dt.float32
BF16 = mybir.dt.bfloat16
I32 = mybir.dt.int32
U32 = mybir.dt.uint32
U16 = mybir.dt.uint16
U8 = mybir.dt.uint8
FP8X4 = mybir.dt.float8_e4m3fn_x4
FP4X4 = mybir.dt.float4_e2m1fn_x4
ADD = mybir.AluOpType.add
MAX = mybir.AluOpType.max
MULT = mybir.AluOpType.mult
IDENT = mybir.ActivationFunctionType.Identity

P = 128
PACK = 4
PASSES = K // (P * PACK)
RUN = 8
HALF = 512
HALVES = S // HALF
PIECES = [(0, 256), (256, 256), (512, 256), (768, 128), (896, 128)]
KIB = 1024
W2_ROW = 4
LAG = 2
A_BANKS = [4, 5, 3, 0, 1, 2]
Y_LAST = [(2, 3), (0, 1), (4, 5)]


def tile_list_pocket_max_affinity_kernel(
    tc, tab_words, tab_scales, offs, w1, w2_words, w2_scales, w3_words, w3_scales, bh, wo, bo, out
):
    nc = tc.nc
    with ExitStack() as ctx:
        keep = ctx.enter_context(tc.tile_pool(name="keep", bufs=1))
        stage = ctx.enter_context(tc.tile_pool(name="stage", bufs=1))
        psum = ctx.enter_context(tc.psum_pool(name="psum", bufs=1))

        def sb(shape, dtype, name):
            return keep.tile(shape, dtype, name=name, align_bytes=64)

        def staged(shape, dtype, name, kib):
            return stage.tile(shape, dtype, name=name, offset=kib * KIB, align_bytes=64)

        def bank(n, name):
            return psum.tile([P, HALF], F32, name=name, offset=2 * KIB * n)

        def load_scales(plane, scales, first, which):
            rows = scales.bitcast(I32).rearrange("a (g r) w -> r g a w", r=4)
            for r in which:
                nc.sync.dma_start(out=plane[first + r : P : 32, :, :].bitcast(I32), in_=rows[r])

        def regroup(dst, src, copy=nc.vector.tensor_copy, dtype=I32):
            copy(
                out=dst[:].bitcast(dtype).rearrange("p a (t q w) -> p a t q w", t=PACK, q=16),
                in_=src[:].bitcast(dtype).rearrange("p a (q t w) -> p a t q w", t=PACK, q=16),
            )

        offsets = keep.tile([P, S // 16], U16, name="offsets")
        nc.sync.dma_start(offsets[:], offs)

        tab_plane = sb([P, T], U8, "tab_plane")
        w2_plane_raw = staged([P, PASSES, H], U8, "w2_plane_raw", 18)
        w3_plane_raw = staged([P, PASSES, H], U8, "w3_plane_raw", 16)
        v_plane_low = sb([P, S], U8, "v_plane_low")
        bh_rows = sb([P, P], F32, "bh_rows")
        w3_raw = sb([P, PASSES, 2 * H], U8, "w3_raw")
        nc.sync.dma_start(out=w3_raw[:].bitcast(I32), in_=w3_words.rearrange("a p b -> p a b").bitcast(I32))
        nc.gpsimd.memset(tab_plane[:, 0 : T // 2].bitcast(I32), 0)
        nc.vector.memset(tab_plane[:, T // 2 : T].bitcast(I32), 0)
        nc.gpsimd.memset(bh_rows[:], 0.0)
        nc.vector.memset(w2_plane_raw[:].bitcast(I32), 0)
        nc.vector.memset(w3_plane_raw[:].bitcast(I32), 0)
        nc.vector.memset(v_plane_low[:].bitcast(I32), 0)
        w2_codes = sb([P, PASSES, 4 * H], U8, "w2_codes")
        w2_plane = sb([P, PASSES, H], U8, "w2_plane")
        nc.vector.memset(w2_codes[:, 0, 0 : PACK * P].bitcast(I32), 0)
        nc.vector.memset(w2_plane[:, 0, :].bitcast(I32), 0)
        identity = sb([P, P], F32, "identity")
        make_identity(nc, identity[:])
        warm = sb([P, 16], F32, "warm")
        nc.vector.memset(warm[:, 0:8], 0.0)
        nc.scalar.activation(warm[:, 8:16], warm[:, 0:8], IDENT)

        tab_scale_rows = tab_scales.bitcast(I32).rearrange("a (g r) w -> r g a w", r=4)
        for r in range(4):
            nc.sync.dma_start(out=tab_plane[r:P:16, :].bitcast(I32), in_=tab_scale_rows[r])
        tab_rows = tab_words.rearrange("a p t i -> a p (t i)").bitcast(I32)
        tab = [staged([P, T], I32, f"tab{a}", 8 * a) for a in range(PASSES)]
        nc.sync.dma_start(out=tab[0][:], in_=tab_rows[0])
        nc.sync.dma_start(
            out=bh_rows[0:PACK, :].rearrange("t (q i) -> t q i", i=RUN),
            in_=bh.rearrange("(q t i) -> t q i", t=PACK, i=RUN),
        )
        load_scales(w3_plane_raw, w3_scales, 0, range(4))
        nc.sync.dma_start(out=tab[1][:], in_=tab_rows[1])

        picks = [offsets[:, s * HALF // 16 : (s + 1) * HALF // 16] for s in range(HALVES)]
        v_plane = sb([P, S], U8, "v_plane")
        nc.vector.tensor_copy(v_plane[:], tab_plane[:].indirect(offsets[:]))
        w2_raw = sb([P, PASSES, 4 * H], U8, "w2_raw")
        nc.sync.dma_start(
            out=w2_raw[:].bitcast(I32), in_=w2_words.rearrange("a p e i -> p a (e i)").bitcast(I32)
        )
        load_scales(w2_plane_raw, w2_scales, W2_ROW, range(3))
        nc.sync.dma_start(out=v_plane_low[0:112, :].bitcast(I32), in_=v_plane[16:P, :].bitcast(I32))
        load_scales(w2_plane_raw, w2_scales, W2_ROW, range(3, 4))
        v_planes = [v_plane, v_plane_low]

        w1_rows = w1.rearrange("(a p j) c -> a p j c", p=P, j=PACK)
        w1_raw = [staged([P, PACK, H], F32, "w1_raw0", 28), staged([P, PACK, H], F32, "w1_raw1", 44)]
        nc.sync.dma_start(out=w1_raw[0][:], in_=w1_rows[0])
        for h in range(2):
            cols = slice(h * H // 2, (h + 1) * H // 2)
            nc.sync.dma_start(out=w1_raw[1][:, :, cols], in_=w1_rows[1][:, :, cols])
        wo_raw = sb([P, PACK, N], F32, "wo_raw")
        wo_rows = wo.rearrange("(q t i) n -> t q i n", t=PACK, i=RUN)
        for t in range(PACK):
            nc.sync.dma_start(out=wo_raw[:, t, :], in_=wo_rows[t])
        bo_col = sb([P, N // P], F32, "bo_col")
        with nc.allow_non_contiguous_dma(reason="one bias value a partition"):
            nc.sync.dma_start(out=bo_col[:], in_=bo.rearrange("(u p) -> p u", p=P))

        bh_turned = bank(7, "bh_turned")
        nc.tensor.transpose(bh_turned[:, 0:P], bh_rows[:], identity[:])
        bh_all = sb([P, PACK], F32, "bh_all")
        nc.scalar.activation(bh_all[:], bh_turned[:, 0:PACK], IDENT)
        bh_cols = [bh_all[:, t : t + 1] for t in range(PACK)]

        v_codes = {}

        def gather_words(a, s, dst):
            v_codes[a, s] = dst
            nc.vector.tensor_copy(dst[:], tab[a][:].bitcast(U32).indirect(picks[s]))

        gather_words(0, 0, sb([P, HALF], U32, "v_codes0_0"))
        gather_words(0, 1, sb([P, HALF], U32, "v_codes0_1"))
        w3_codes = sb([P, PASSES, 2 * H], U8, "w3_codes")
        w3_plane = sb([P, PASSES, H], U8, "w3_plane")
        regroup(w3_codes, w3_raw, nc.scalar.copy, U32)
        acc_warm = bank(6, "acc_warm")
        for n in range(5):
            nc.tensor.matmul_mx(
                out=acc_warm[:],
                lhsT=w2_codes[:, 0, 0 : PACK * P].bitcast(FP8X4),
                lhsT_scale=w2_plane[:, 0, 0:P],
                rhs=w3_codes[:, 0, :].bitcast(FP4X4),
                rhs_scale=w2_plane[:, 0, :],
                start=True,
                stop=True,
            )

        regroup(w3_plane, w3_plane_raw, nc.scalar.copy, U32)
        gather_words(1, 0, sb([P, HALF], U32, "v_codes1_0"))
        regroup(w2_codes, w2_raw)
        regroup(w2_plane, w2_plane_raw)
        gather_words(1, 1, staged([P, HALF], U32, "v_codes1_1", 18))

        def product(acc, codes, plane, a, j0, width):
            s, c0 = divmod(j0, HALF)
            nc.tensor.matmul_mx(
                out=acc[:, :width],
                lhsT=codes,
                lhsT_scale=plane,
                rhs=v_codes[a, s][:, c0 : c0 + width].bitcast(FP8X4),
                rhs_scale=v_planes[a][:, j0 : j0 + width],
                start=(a == 0),
                stop=(a == PASSES - 1),
            )

        acc_b, acc_c, b_sb, bc_sb = {}, {}, {}, {}

        def b_pass(a, s, t):
            if a == 0:
                acc_b[s, t] = bank(PACK * s + t, f"acc_b{s}_{t}")
            product(
                acc_b[s, t],
                w3_codes[:, a, t * 256 : (t + 1) * 256].bitcast(FP4X4),
                w3_plane[:, a, t * P : (t + 1) * P],
                a, s * HALF, HALF,
            )

        def b_out(s, t, dst):
            b_sb[s, t] = dst
            nc.scalar.activation(dst[:], acc_b[s, t][:], IDENT, bias=bh_cols[t])

        def c_pass(a, s, t, where):
            if a == 0:
                acc_c[s, t] = bank(where, f"acc_c{s}_{t}")
            product(
                acc_c[s, t],
                w2_codes[:, a, t * 512 : (t + 1) * 512].bitcast(FP8X4),
                w2_plane[W2_ROW:P, a, t * P : (t + 1) * P],
                a, s * HALF, HALF,
            )

        def c_out(s, t, dst):
            bc_sb[s, t] = dst
            nc.vector.scalar_tensor_tensor(dst, acc_c[s, t][:], bh_cols[t], b_sb[s, t][:], ADD, MAX)

        shared = sb([P, PACK * HALF], F32, "shared")
        w1_bf = staged([P, PACK * PASSES * H], BF16, "w1_bf", 60)
        w1_codes = sb([P, PACK * PASSES * P], U32, "w1_codes")
        w1_plane = sb([P, PACK * PASSES * P], U8, "w1_plane")

        def cast_views(a):
            src = w1_raw[a][:].rearrange("p j (q t i) -> p q t i j", t=PACK, i=RUN)
            dst = w1_bf[:].rearrange("p (t a q i j) -> p a q t i j", t=PACK, a=PASSES, i=RUN, j=PACK)[:, a]
            return src, dst

        def cast_on_gpsimd(a, t0):
            src, dst = cast_views(a)
            nc.gpsimd.tensor_scalar(
                out=dst[:, :, t0:PACK], in0=src[:, :, t0:PACK], scalar1=1.0, scalar2=0.0, op0=MULT, op1=ADD
            )

        def cast_on_scalar(a, t):
            src, dst = cast_views(a)
            order = "p q (h i) j -> p q h j i"
            nc.scalar.copy(out=dst[:, :, t].rearrange(order, h=2), in_=src[:, :, t].rearrange(order, h=2))

        def cast_half_on_scalar(h, t0, t1):
            src, dst = cast_views(1)
            order = "p q t i j -> p q t j i"
            blocks = slice(8 * h, 8 * h + 8)
            nc.scalar.copy(out=dst[:, blocks, t0:t1].rearrange(order), in_=src[:, blocks, t0:t1].rearrange(order))

        def quantize_w1(pair):
            c0, c1 = 2 * PASSES * P * pair, 2 * PASSES * P * (pair + 1)
            nc.vector.quantize_mx(
                out=w1_codes[:, c0:c1].bitcast(FP8X4), scales=w1_plane[:, c0:c1], in_=w1_bf[:, PACK * c0 : PACK * c1]
            )

        def a_pass(acc, a, t, j0, width):
            c0 = (PASSES * t + a) * P
            product(acc, w1_codes[:, c0 : c0 + P].bitcast(FP8X4), w1_plane[:, c0 : c0 + P], a, j0, width)

        def c_passes(s, t, where):
            for a in range(PASSES):
                c_pass(a, s, t, where)

        def b_end(s, t, dst):
            b_pass(1, s, t)
            b_out(s, t, dst)

        def high(t):
            return shared[:, t * HALF : (t + 1) * HALF]

        for s in range(HALVES):
            for t in range(PACK - s):
                b_pass(0, s, t)
        for t in range(PACK):
            b_end(0, t, sb([P, HALF], F32, f"b_sb0_{t}"))
        for t in range(PACK):
            c_passes(0, t, (t - 1) % 8)
            c_out(0, t, sb([P, HALF], F32, f"bc_sb0_{t}")[:])
            if t in (1, 2):
                b_end(1, t - 1, sb([P, HALF], F32, f"b_sb1_{t - 1}"))
        cast_on_scalar(0, 0)
        cast_on_gpsimd(0, 1)
        cast_half_on_scalar(0, 0, 3)
        cast_half_on_scalar(1, 0, 2)
        cast_half_on_scalar(1, 2, 3)
        cast_on_gpsimd(1, 3)
        for t in range(2):
            c_passes(1, t, 3 - 3 * t)
            c_out(1, t, high(t))
        quantize_w1(0)
        quantize_w1(1)
        for t in range(2, PACK):
            if t == 3:
                b_pass(0, 1, t)
            b_end(1, t, staged([P, HALF], F32, f"b_sb1_{t}", 44 + 2 * t))
        for t in range(2, PACK):
            c_passes(1, t, t - 1)
            c_out(1, t, high(t))

        wo_bf = staged([P, N, PACK], BF16, "wo_bf", 60)
        wo_codes = sb([P, N], U32, "wo_codes")
        wo_plane = sb([P, N], U8, "wo_plane")
        nc.gpsimd.tensor_scalar(
            out=wo_bf[:], in0=wo_raw[:].rearrange("p t n -> p n t"), scalar1=1.0, scalar2=0.0, op0=MULT, op1=ADD
        )

        out_rows = out.rearrange("(u p) s -> p u s", p=P)

        def second_product(n, h_rows):
            j0, width = PIECES[n]
            h_bf = sb([P, width, PACK], BF16, f"h_bf{n}")
            last = n >= len(PIECES) - 2
            final = n == len(PIECES) - 1
            woven = h_bf[:].rearrange("p (c i) t -> p c t i", i=4)
            rows_in = h_rows[:].rearrange("p t (c i) -> p c t i", i=4)
            if final:
                other = bc_high[:, :, j0 - HALF : j0 - HALF + width].rearrange("p t (c i) -> p c t i", i=4)
                nc.vector.tensor_tensor(woven, rows_in, other, MAX)
            else:
                (nc.vector.tensor_copy if last else nc.scalar.copy)(out=woven, in_=rows_in)
            h_codes = sb([P, width], U32, f"h_codes{n}")
            h_plane = sb([P, width], U8, f"h_plane{n}")
            nc.vector.quantize_mx(
                out=h_codes[:].bitcast(FP8X4), scales=h_plane[:], in_=h_bf[:].rearrange("p n t -> p (n t)")
            )
            y = sb([P, N // P, width], F32, f"y{n}")
            accs = []
            for u in range(N // P):
                if n >= 2:
                    accs.append(bank(Y_LAST[n - 2][u], f"acc_y{n}_{u}")[:, 0:width])
                else:
                    if u == 0:
                        both = bank(6 + n % 2, f"acc_y{n}")
                    accs.append(both[:, u * width : (u + 1) * width])
                nc.tensor.matmul_mx(
                    out=accs[u],
                    lhsT=wo_codes[:, u * P : (u + 1) * P].bitcast(FP8X4),
                    lhsT_scale=wo_plane[:, u * P : (u + 1) * P],
                    rhs=h_codes[:].bitcast(FP8X4),
                    rhs_scale=h_plane[:],
                    start=True,
                    stop=True,
                )
            for u in range(N // P):
                if n >= 2 and u == 1:
                    nc.vector.tensor_scalar_add(y[:, u, :], accs[u], bo_col[:, u : u + 1])
                else:
                    nc.scalar.activation(y[:, u, :], accs[u], IDENT, bias=bo_col[:, u : u + 1])
            nc.sync.dma_start(out=out_rows[:, :, j0 : j0 + width], in_=y[:])

        def third_pocket(n):
            j0, width = PIECES[n]
            s, c0 = divmod(j0, HALF)
            h_rows = sb([P, PACK, width], BF16, f"h_rows{n}")
            accs = [bank(A_BANKS[(PACK * n + t) % len(A_BANKS)], f"acc_a{n}_{t}") for t in range(PACK)]

            for t in range(PACK):
                for a in range(PASSES):
                    a_pass(accs[t], a, t, j0, width)
                nc.vector.scalar_tensor_tensor(
                    h_rows[:, t, :], accs[t][:, :width], bh_cols[t], bc_sb[s, t][:, c0 : c0 + width], ADD, MAX
                )
            return h_rows

        def early_piece(n):
            j0, width = PIECES[n]
            a_rows = sb([P, PACK, width], F32, "a_rows")
            acc = bank(7, "acc_early")
            for t in range(PACK):
                for a in range(PASSES):
                    a_pass(acc[:, t * width : (t + 1) * width], a, t, j0, width)
            for t in range(PACK):
                nc.scalar.activation(a_rows[:, t, :], acc[:, t * width : (t + 1) * width], IDENT, bias=bh_cols[t])
            return a_rows

        bc_high = shared[:, 0 : PACK * HALF].rearrange("p (t n) -> p t n", t=PACK)
        rows = {}
        for n in range(len(PIECES) + LAG):
            if n < len(PIECES) - 1:
                rows[n] = third_pocket(n)
            if n == 0:
                rows[len(PIECES) - 1] = early_piece(len(PIECES) - 1)
            if n == LAG:
                nc.vector.quantize_mx(
                    out=wo_codes[:].bitcast(FP8X4), scales=wo_plane[:], in_=wo_bf[:].rearrange("p n t -> p (n t)")
                )
            if n >= LAG:
                second_product(n - LAG, rows[n - LAG])
